import numpy as np
import ml_dtypes


def mxq(x, axis, fmt="e4m3"):
    dtype, down = {"e4m3": (ml_dtypes.float8_e4m3fn, 7), "e5m2": (ml_dtypes.float8_e5m2, 14)}[fmt]
    v = np.moveaxis(np.asarray(x, np.float32).astype(ml_dtypes.bfloat16).astype(np.float64), axis, -1)
    blocks = v.reshape(v.shape[:-1] + (-1, 32))
    amax = np.abs(blocks).max(-1, keepdims=True)
    byte = np.maximum(np.where(amax > 0, np.frexp(amax)[1] - 1 + 127, 0) - down, 1)
    scale = np.exp2(byte - 127.0)
    codes = (blocks / scale).astype(np.float32).astype(dtype).astype(np.float64)
    return np.moveaxis((codes * scale).reshape(v.shape), -1, axis)


WIDE = False


def mx_kscale(k):
    if not WIDE:
        return np.ones(k)
    levels = np.array([10, -10, 5, -5, 0])
    if k % 512:
        return np.exp2(np.random.permutation(np.resize(levels, k // 32))).repeat(32)
    a = np.empty((k // 512, 16))
    for p in range(k // 512):
        a[p, :8] = np.random.permutation(np.resize(levels, 8))
        for g in range(8):
            far = levels[np.abs(levels - a[p, g]) >= 10]
            a[p, g + 8] = far[np.random.randint(len(far))]
    return np.exp2(a.ravel()).repeat(32)


def f64(x):
    return np.asarray(x).astype(np.float64)


def striped(idx):
    return np.tile(idx.reshape(-1, 16).T, (8, 1)).astype(np.uint16)


def unstriped(offs):
    return offs[:16].T.reshape(-1).astype(np.int64)


E2M1 = np.array([0.0, 0.5, 1.0, 1.5, 2.0, 3.0, 4.0, 6.0, -0.0, -0.5, -1.0, -1.5, -2.0, -3.0, -4.0, -6.0])


def pack_weight(w, fmt):
    k, n = w.shape
    w = f64(np.asarray(w, np.float32).astype(ml_dtypes.bfloat16)).reshape(k // 32, 32, n)
    amax = np.abs(w).max(1)
    if fmt == "e4m3":
        byte = np.frexp(amax)[1] - 1 + 127 - 7
    else:
        mant, ex = np.frexp(amax / 6.0)
        byte = np.where(mant > 0.5, ex, ex - 1) + 127
    byte = np.clip(np.where(amax > 0, byte, 1), 1, 254)
    scaled = (w * np.exp2(127.0 - byte)[:, None, :]).reshape(k, n).astype(np.float32)
    by_word = np.ascontiguousarray(scaled.reshape(k // 512, 128, 4, n).transpose(0, 1, 3, 2))
    if fmt == "e4m3":
        words = by_word.astype(ml_dtypes.float8_e4m3fn).view(np.uint8)
    else:
        c = by_word.astype(ml_dtypes.float4_e2m1fn).view(np.uint8) & 0xF
        words = (c[..., 0::2] | (c[..., 1::2] << 4)).reshape(k // 512, 128, 2 * n)
    return np.ascontiguousarray(words), np.ascontiguousarray(byte.astype(np.uint8).reshape(k // 512, 16, n))


def unpack_weight(words, scales, fmt):
    g, _, n = scales.shape
    words = np.ascontiguousarray(words).reshape(g, 128, n, -1)
    if fmt == "e4m3":
        vals = words.view(ml_dtypes.float8_e4m3fn).astype(np.float64)
    else:
        nib = np.empty((g, 128, n, 4), np.uint8)
        nib[..., 0::2] = words & 0xF
        nib[..., 1::2] = words >> 4
        vals = E2M1[nib]
    vals = vals * np.repeat(np.exp2(scales.astype(np.float64) - 127.0), 8, axis=1)[..., None]
    return vals.transpose(0, 1, 3, 2).reshape(g * 512, n)


def split(x):
    m, e = np.frexp(f64(x))
    hi = np.ldexp(np.trunc(16.0 * m) / 16.0, e)
    return hi, f64(x) - hi


def silu(v):
    return v / (1.0 + np.exp(-np.maximum(v, -700.0)))


K, M, T, S = 1536, 128, 4096, 2048


def setup_inputs():
    n = np.random.standard_normal
    s = mx_kscale(K)[:, None]
    v = pack_weight(n((K, T)) * s, "e4m3")
    return {
        "tab_words": v[0],
        "tab_scales": v[1],
        "w": (n((K, M)) / np.sqrt(K) / s).astype(np.float32),
        "ts": np.tile(np.exp(0.5 * n(T)), (128, 1)).astype(np.float32),
        "b": (0.3 * n(128)).astype(np.float32),
        "offs": striped(np.random.permutation(T)[:S]),
    }


def reference(tab_words, tab_scales, w, ts, b, offs):
    tab_ = unpack_weight(tab_words, tab_scales, "e4m3")[:, unstriped(offs)]
    w_hi, w_lo = split(w)
    w_hi_, w_lo_ = mxq(w_hi, 0, "e4m3"), mxq(w_lo, 0, "e4m3")
    y = w_hi_.T @ tab_ + w_lo_.T @ tab_
    y = y * f64(ts)[0][unstriped(offs)]
    return silu(y + f64(b)[:, None])

@@ -1,0 +1,129 @@
+from contextlib import ExitStack
+
+import concourse.mybir as mybir
+
+K, M, T, S = 1536, 128, 4096, 2048
+FLOPS = 2 * 2 * K * M * S
+
+F32 = mybir.dt.float32
+BF16 = mybir.dt.bfloat16
+I32 = mybir.dt.int32
+U32 = mybir.dt.uint32
+U16 = mybir.dt.uint16
+U8 = mybir.dt.uint8
+FP8X4 = mybir.dt.float8_e4m3fn_x4
+ALU = mybir.AluOpType
+ACT = mybir.ActivationFunctionType
+
+P = 128
+PACK = 4
+K_PASS = P * PACK
+PASSES = K // K_PASS
+N_TILE = 512
+BANKS = S // N_TILE
+PER_COL = 16
+HI_MASK = -(1 << 20)
+OUT_WIDTHS = (512, 512, 512, 256, 128, 128)
+
+
+def tile_list_tabts_silu_kernel(tc, tab_words, tab_scales, w, ts, b, offs, out):
+    nc = tc.nc
+    with ExitStack() as ctx:
+        keep = ctx.enter_context(tc.tile_pool(name="keep", bufs=1))
+        psum = ctx.enter_context(tc.psum_pool(name="psum", bufs=1))
+
+        offsets = keep.tile([P, S // PER_COL], U16, name="offsets")
+        scale_window = keep.tile([P, T // 4], I32, name="scale_window", align_bytes=64)
+        nc.vector.memset(scale_window[:], 0)
+
+        w_raw = [keep.tile([P, PACK, M], F32, name=f"w_raw{a}", align_bytes=64) for a in range(PASSES)]
+        for a in range(PASSES):
+            rows = w[a * K_PASS : (a + 1) * K_PASS, :]
+            nc.sync.dma_start(out=w_raw[a][:], in_=rows.rearrange("(p i) n -> p i n", i=PACK))
+        nc.sync.dma_start(offsets[:], offs)
+        bias = keep.tile([P, 1], F32, name="bias")
+        nc.sync.dma_start(out=bias[:], in_=b.rearrange("(p o) -> p o", o=1))
+        for q in range(4):
+            nc.sync.dma_start(
+                out=scale_window[32 * q : 32 * q + 4 * PASSES, :],
+                in_=tab_scales[:, 4 * q : 4 * q + 4, :].bitcast(I32),
+            )
+        word_window = [keep.tile([P, T], I32, name=f"word_window{a}", align_bytes=64) for a in range(PASSES)]
+        for a in range(PASSES):
+            nc.sync.dma_start(
+                out=word_window[a][:],
+                in_=tab_words[a].rearrange("p t i -> p (t i)").bitcast(I32),
+            )
+        ts_window = keep.tile([P, T], F32, name="ts_window", align_bytes=64)
+        nc.sync.dma_start(out=ts_window[:], in_=ts)
+
+        w_hi = [keep.tile([P, PACK, M], I32, name=f"w_hi{a}", align_bytes=64) for a in range(PASSES)]
+        w_bf = [keep.tile([P, 2, M, PACK], BF16, name=f"w_bf{a}", align_bytes=64) for a in range(PASSES)]
+        w_codes = [keep.tile([P, 2 * M], U32, name=f"w_codes{a}", align_bytes=64) for a in range(PASSES)]
+        w_scales = [keep.tile([P, 2 * M], U8, name=f"w_scales{a}", align_bytes=64) for a in range(PASSES)]
+        for a in range(PASSES):
+            nc.vector.tensor_scalar(
+                out=w_hi[a][:], in0=w_raw[a][:].bitcast(I32), scalar1=HI_MASK, scalar2=None, op0=ALU.bitwise_and
+            )
+        for a in range(PASSES):
+            hi = w_hi[a][:].bitcast(F32).rearrange("p i n -> p n i")
+            nc.scalar.activation(out=w_bf[a][:, 0], in_=hi, func=ACT.Copy)
+            nc.vector.tensor_tensor(
+                out=w_bf[a][:, 1], in0=w_raw[a][:].rearrange("p i n -> p n i"), in1=hi, op=ALU.subtract
+            )
+        for a in range(PASSES):
+            nc.vector.quantize_mx(
+                out=w_codes[a][:].bitcast(FP8X4),
+                scales=w_scales[a][:],
+                in_=w_bf[a][:].rearrange("p h n i -> p (h n i)"),
+            )
+
+        picked_scales = keep.tile([P, S], U8, name="picked_scales", align_bytes=64)
+        nc.vector.tensor_copy(picked_scales[:], scale_window[:].bitcast(U8).indirect(offsets[:]))
+
+        picked = [keep.tile([P, S], U32, name=f"picked{a}", align_bytes=64) for a in range(PASSES)]
+        acc = [psum.tile([M, N_TILE], F32, name=f"acc{c}") for c in range(BANKS)]
+        sums = keep.tile([M, S], F32, name="sums", align_bytes=64)
+
+        def list_slice(start, width):
+            return offsets[:, start // PER_COL : (start + width) // PER_COL]
+
+        def multiply(a, c):
+            cols = slice(c * N_TILE, (c + 1) * N_TILE)
+            for h in range(2):
+                w_cols = slice(h * M, (h + 1) * M)
+                nc.tensor.matmul_mx(
+                    out=acc[c][:],
+                    lhsT=w_codes[a][:, w_cols].bitcast(FP8X4),
+                    lhsT_scale=w_scales[a][:, w_cols],
+                    rhs=picked[a][:, cols].bitcast(FP8X4),
+                    rhs_scale=picked_scales[4 * a :, cols],
+                    start=(a == 0 and h == 0),
+                    stop=(a == PASSES - 1 and h == 1),
+                )
+
+        for a in range(PASSES - 1):
+            nc.vector.tensor_copy(picked[a][:], word_window[a][:].bitcast(U32).indirect(offsets[:]))
+            for c in range(BANKS):
+                multiply(a, c)
+        last = PASSES - 1
+        for c in range(BANKS):
+            cols = slice(c * N_TILE, (c + 1) * N_TILE)
+            nc.vector.tensor_copy(
+                picked[last][:, cols],
+                word_window[last][:].bitcast(U32).indirect(list_slice(c * N_TILE, N_TILE)),
+            )
+            multiply(last, c)
+            nc.scalar.activation(out=sums[:, cols], in_=acc[c][:], func=ACT.Copy)
+
+        scaled = keep.tile([M, S], F32, name="scaled", align_bytes=64)
+        result = keep.tile([M, S], F32, name="result", align_bytes=64)
+        start = 0
+        for width in OUT_WIDTHS:
+            cols = slice(start, start + width)
+            nc.vector.tensor_tensor(
+                scaled[:, cols], ts_window[:].indirect(list_slice(start, width)), sums[:, cols], ALU.mult
+            )
+            nc.scalar.activation(out=result[:, cols], in_=scaled[:, cols], func=ACT.Silu, bias=bias[:])
+            nc.sync.dma_start(out=out[:, cols], in_=result[:, cols])
+            start += width

@@ -1,6 +1,7 @@
 from contextlib import ExitStack
 
 import concourse.mybir as mybir
+from concourse.masks import make_identity
 
 K, M, T, S = 1536, 128, 4096, 2048
 FLOPS = 2 * 2 * K * M * S
@@ -23,6 +24,7 @@ N_TILE = 512
 BANKS = S // N_TILE
 PER_COL = 16
 HI_MASK = -(1 << 20)
+GATHER_WIDTHS = (2048, 1024, 512)
 OUT_WIDTHS = (512, 512, 512, 256, 128, 128)
 
 
@@ -31,6 +33,8 @@ def tile_list_tabts_silu_kernel(tc, tab_words, tab_scales, w, ts, b, offs, out):
     with ExitStack() as ctx:
         keep = ctx.enter_context(tc.tile_pool(name="keep", bufs=1))
         psum = ctx.enter_context(tc.psum_pool(name="psum", bufs=1))
+
+        spread_pool = ctx.enter_context(tc.psum_pool(name="spread", bufs=4))
 
         offsets = keep.tile([P, S // PER_COL], U16, name="offsets")
         scale_window = keep.tile([P, T // 4], I32, name="scale_window", align_bytes=64)
@@ -49,13 +53,14 @@ def tile_list_tabts_silu_kernel(tc, tab_words, tab_scales, w, ts, b, offs, out):
                 in_=tab_scales[:, 4 * q : 4 * q + 4, :].bitcast(I32),
             )
         word_window = [keep.tile([P, T], I32, name=f"word_window{a}", align_bytes=64) for a in range(PASSES)]
+        ts_rows = keep.tile([P, T // P], F32, name="ts_rows", align_bytes=64)
         for a in range(PASSES):
             nc.sync.dma_start(
                 out=word_window[a][:],
                 in_=tab_words[a].rearrange("p t i -> p (t i)").bitcast(I32),
             )
-        ts_window = keep.tile([P, T], F32, name="ts_window", align_bytes=64)
-        nc.sync.dma_start(out=ts_window[:], in_=ts)
+            if a == 0:
+                nc.sync.dma_start(out=ts_rows[:], in_=ts[0].rearrange("(p c) -> p c", p=P))
 
         w_hi = [keep.tile([P, PACK, M], I32, name=f"w_hi{a}", align_bytes=64) for a in range(PASSES)]
         w_bf = [keep.tile([P, 2, M, PACK], BF16, name=f"w_bf{a}", align_bytes=64) for a in range(PASSES)]
@@ -81,6 +86,17 @@ def tile_list_tabts_silu_kernel(tc, tab_words, tab_scales, w, ts, b, offs, out):
         picked_scales = keep.tile([P, S], U8, name="picked_scales", align_bytes=64)
         nc.vector.tensor_copy(picked_scales[:], scale_window[:].bitcast(U8).indirect(offsets[:]))
 
+        identity = keep.tile([P, P], F32, name="identity", align_bytes=64)
+        make_identity(nc, identity[:])
+        ts_window = keep.tile([P, T], F32, name="ts_window", align_bytes=64)
+        ts_by_row = ts_window[:].rearrange("p (r c) -> p r c", r=P)
+        for c0 in range(0, T // P, 4):
+            spread = spread_pool.tile([P, 4, P], F32, name="spread")
+            for j in range(4):
+                column = ts_rows[:, c0 + j : c0 + j + 1]
+                nc.tensor.transpose(spread[:, j, :], column.to_broadcast([P, P]), identity[:])
+            nc.scalar.copy(out=ts_by_row[:, :, c0 : c0 + 4], in_=spread[:].rearrange("p j r -> p r j"))
+
         picked = [keep.tile([P, S], U32, name=f"picked{a}", align_bytes=64) for a in range(PASSES)]
         acc = [psum.tile([M, N_TILE], F32, name=f"acc{c}") for c in range(BANKS)]
         sums = keep.tile([M, S], F32, name="sums", align_bytes=64)
@@ -102,19 +118,17 @@ def tile_list_tabts_silu_kernel(tc, tab_words, tab_scales, w, ts, b, offs, out):
                     stop=(a == PASSES - 1 and h == 1),
                 )
 
-        for a in range(PASSES - 1):
-            nc.vector.tensor_copy(picked[a][:], word_window[a][:].bitcast(U32).indirect(offsets[:]))
-            for c in range(BANKS):
-                multiply(a, c)
-        last = PASSES - 1
-        for c in range(BANKS):
-            cols = slice(c * N_TILE, (c + 1) * N_TILE)
-            nc.vector.tensor_copy(
-                picked[last][:, cols],
-                word_window[last][:].bitcast(U32).indirect(list_slice(c * N_TILE, N_TILE)),
-            )
-            multiply(last, c)
-            nc.scalar.activation(out=sums[:, cols], in_=acc[c][:], func=ACT.Copy)
+        for a, width in enumerate(GATHER_WIDTHS):
+            for start in range(0, S, width):
+                nc.vector.tensor_copy(
+                    picked[a][:, start : start + width],
+                    word_window[a][:].bitcast(U32).indirect(list_slice(start, width)),
+                )
+                for c in range(start // N_TILE, (start + width) // N_TILE):
+                    multiply(a, c)
+                    if a == PASSES - 1:
+                        cols = slice(c * N_TILE, (c + 1) * N_TILE)
+                        nc.scalar.activation(out=sums[:, cols], in_=acc[c][:], func=ACT.Copy)
 
         scaled = keep.tile([M, S], F32, name="scaled", align_bytes=64)
         result = keep.tile([M, S], F32, name="result", align_bytes=64)

@@ -24,6 +24,7 @@ N_TILE = 512
 BANKS = S // N_TILE
 PER_COL = 16
 HI_MASK = -(1 << 20)
+SIGN_BIT = -(1 << 31)
 GATHER_WIDTHS = (2048, 1024, 512)
 OUT_WIDTHS = (512, 512, 512, 256, 128, 128)
 
@@ -33,12 +34,13 @@ def tile_list_tabts_silu_kernel(tc, tab_words, tab_scales, w, ts, b, offs, out):
     with ExitStack() as ctx:
         keep = ctx.enter_context(tc.tile_pool(name="keep", bufs=1))
         psum = ctx.enter_context(tc.psum_pool(name="psum", bufs=1))
-
-        spread_pool = ctx.enter_context(tc.psum_pool(name="spread", bufs=4))
+        turn = ctx.enter_context(tc.psum_pool(name="turn", bufs=4))
 
         offsets = keep.tile([P, S // PER_COL], U16, name="offsets")
-        scale_window = keep.tile([P, T // 4], I32, name="scale_window", align_bytes=64)
+        scale_window = keep.tile([P, T // 4], I32, name="scale_window", tag="reused", align_bytes=64)
         nc.vector.memset(scale_window[:], 0)
+        planes = keep.tile([P, PASSES, S // 4], I32, name="planes", align_bytes=64)
+        nc.vector.memset(planes[:].rearrange("p a s -> p (a s)"), 0)
 
         w_raw = [keep.tile([P, PACK, M], F32, name=f"w_raw{a}", align_bytes=64) for a in range(PASSES)]
         for a in range(PASSES):
@@ -47,55 +49,69 @@ def tile_list_tabts_silu_kernel(tc, tab_words, tab_scales, w, ts, b, offs, out):
         nc.sync.dma_start(offsets[:], offs)
         bias = keep.tile([P, 1], F32, name="bias")
         nc.sync.dma_start(out=bias[:], in_=b.rearrange("(p o) -> p o", o=1))
-        for q in range(4):
-            nc.sync.dma_start(
-                out=scale_window[32 * q : 32 * q + 4 * PASSES, :],
-                in_=tab_scales[:, 4 * q : 4 * q + 4, :].bitcast(I32),
-            )
-        word_window = [keep.tile([P, T], I32, name=f"word_window{a}", align_bytes=64) for a in range(PASSES)]
-        ts_rows = keep.tile([P, T // P], F32, name="ts_rows", align_bytes=64)
-        for a in range(PASSES):
-            nc.sync.dma_start(
-                out=word_window[a][:],
-                in_=tab_words[a].rearrange("p t i -> p (t i)").bitcast(I32),
-            )
-            if a == 0:
-                nc.sync.dma_start(out=ts_rows[:], in_=ts[0].rearrange("(p c) -> p c", p=P))
+        scale_rows = tab_scales.rearrange("a q t -> (a q) t").bitcast(I32)
+        nc.sync.dma_start(out=scale_window[0:32, :], in_=scale_rows[0:32, :])
+        nc.sync.dma_start(out=scale_window[64:P:4, :], in_=scale_rows[32:48, :])
 
-        w_hi = [keep.tile([P, PACK, M], I32, name=f"w_hi{a}", align_bytes=64) for a in range(PASSES)]
+        def load_words(a, window):
+            nc.sync.dma_start(out=window[:], in_=tab_words[a].rearrange("p t i -> p (t i)").bitcast(I32))
+
+        word_window = [keep.tile([P, T], I32, name=f"word_window{a}", align_bytes=64) for a in range(PASSES - 1)]
+        load_words(0, word_window[0])
+        ts_rows = keep.tile([P, T // P], F32, name="ts_rows", align_bytes=64)
+        nc.sync.dma_start(out=ts_rows[:], in_=ts[0].rearrange("(p c) -> p c", p=P))
+        load_words(1, word_window[1])
+
+        identity = keep.tile([P, P], F32, name="identity", align_bytes=64)
+        make_identity(nc, identity[:])
+
+        neg_hi = [keep.tile([P, PACK, M], I32, name=f"neg_hi{a}", align_bytes=64) for a in range(PASSES)]
+        lo_turned = [keep.tile([M, PACK, P], F32, name=f"lo_turned{a}", align_bytes=64) for a in range(PASSES)]
         w_bf = [keep.tile([P, 2, M, PACK], BF16, name=f"w_bf{a}", align_bytes=64) for a in range(PASSES)]
         w_codes = [keep.tile([P, 2 * M], U32, name=f"w_codes{a}", align_bytes=64) for a in range(PASSES)]
         w_scales = [keep.tile([P, 2 * M], U8, name=f"w_scales{a}", align_bytes=64) for a in range(PASSES)]
         for a in range(PASSES):
             nc.vector.tensor_scalar(
-                out=w_hi[a][:], in0=w_raw[a][:].bitcast(I32), scalar1=HI_MASK, scalar2=None, op0=ALU.bitwise_and
+                out=neg_hi[a][:], in0=w_raw[a][:].bitcast(I32), scalar1=HI_MASK, scalar2=SIGN_BIT,
+                op0=ALU.bitwise_and, op1=ALU.bitwise_xor,
             )
         for a in range(PASSES):
-            hi = w_hi[a][:].bitcast(F32).rearrange("p i n -> p n i")
-            nc.scalar.activation(out=w_bf[a][:, 0], in_=hi, func=ACT.Copy)
-            nc.vector.tensor_tensor(
-                out=w_bf[a][:, 1], in0=w_raw[a][:].rearrange("p i n -> p n i"), in1=hi, op=ALU.subtract
-            )
+            neg = neg_hi[a][:].bitcast(F32)
+            bank = turn.tile([P, PACK, P], F32, name="bank")
+            for i in range(PACK):
+                nc.tensor.matmul(bank[:, i, :], w_raw[a][:, i, :], identity[:], start=True, stop=False, is_transpose=True)
+                nc.tensor.matmul(bank[:, i, :], neg[:, i, :], identity[:], start=False, stop=True, is_transpose=True)
+            nc.scalar.copy(out=lo_turned[a][:], in_=bank[:])
+            nc.scalar.activation(out=w_bf[a][:, 0], in_=neg.rearrange("p i n -> p n i"), func=ACT.Copy, scale=-1.0)
         for a in range(PASSES):
-            nc.vector.quantize_mx(
-                out=w_codes[a][:].bitcast(FP8X4),
-                scales=w_scales[a][:],
-                in_=w_bf[a][:].rearrange("p h n i -> p (h n i)"),
-            )
+            bank = turn.tile([P, PACK, P], F32, name="bank")
+            for i in range(PACK):
+                nc.tensor.transpose(bank[:, i, :], lo_turned[a][:, i, :], identity[:])
+            nc.scalar.activation(out=w_bf[a][:, 1], in_=bank[:].rearrange("p i n -> p n i"), func=ACT.Copy)
 
-        picked_scales = keep.tile([P, S], U8, name="picked_scales", align_bytes=64)
-        nc.vector.tensor_copy(picked_scales[:], scale_window[:].bitcast(U8).indirect(offsets[:]))
+        picked_rows = keep.tile([P, S], U8, name="picked_rows", align_bytes=64)
+        nc.vector.tensor_copy(picked_rows[:], scale_window[:].bitcast(U8).indirect(offsets[:]))
+        last_window = keep.tile([P, T], I32, name="last_window", tag="reused", align_bytes=64)
+        word_window.append(last_window)
+        for a in range(PASSES):
+            first, step = ((0, 1), (16, 1), (64, 4))[a]
+            for r in range(4):
+                nc.sync.dma_start(
+                    out=planes[32 * r : 32 * r + 4, a, :],
+                    in_=picked_rows[first + 4 * step * r : first + 4 * step * (r + 1) : step, :].bitcast(I32),
+                )
+            if a == 0:
+                load_words(PASSES - 1, last_window)
+        picked_scales = planes[:].bitcast(U8)
 
-        identity = keep.tile([P, P], F32, name="identity", align_bytes=64)
-        make_identity(nc, identity[:])
         ts_window = keep.tile([P, T], F32, name="ts_window", align_bytes=64)
         ts_by_row = ts_window[:].rearrange("p (r c) -> p r c", r=P)
         for c0 in range(0, T // P, 4):
-            spread = spread_pool.tile([P, 4, P], F32, name="spread")
+            bank = turn.tile([P, 4, P], F32, name="bank")
             for j in range(4):
                 column = ts_rows[:, c0 + j : c0 + j + 1]
-                nc.tensor.transpose(spread[:, j, :], column.to_broadcast([P, P]), identity[:])
-            nc.scalar.copy(out=ts_by_row[:, :, c0 : c0 + 4], in_=spread[:].rearrange("p j r -> p r j"))
+                nc.tensor.transpose(bank[:, j, :], column.to_broadcast([P, P]), identity[:])
+            nc.scalar.copy(out=ts_by_row[:, :, c0 : c0 + 4], in_=bank[:].rearrange("p j r -> p r j"))
 
         picked = [keep.tile([P, S], U32, name=f"picked{a}", align_bytes=64) for a in range(PASSES)]
         acc = [psum.tile([M, N_TILE], F32, name=f"acc{c}") for c in range(BANKS)]
@@ -113,7 +129,7 @@ def tile_list_tabts_silu_kernel(tc, tab_words, tab_scales, w, ts, b, offs, out):
                     lhsT=w_codes[a][:, w_cols].bitcast(FP8X4),
                     lhsT_scale=w_scales[a][:, w_cols],
                     rhs=picked[a][:, cols].bitcast(FP8X4),
-                    rhs_scale=picked_scales[4 * a :, cols],
+                    rhs_scale=picked_scales[:, a, cols],
                     start=(a == 0 and h == 0),
                     stop=(a == PASSES - 1 and h == 1),
                 )
@@ -124,6 +140,13 @@ def tile_list_tabts_silu_kernel(tc, tab_words, tab_scales, w, ts, b, offs, out):
                     picked[a][:, start : start + width],
                     word_window[a][:].bitcast(U32).indirect(list_slice(start, width)),
                 )
+                if a == 0:
+                    for g in range(PASSES):
+                        nc.vector.quantize_mx(
+                            out=w_codes[g][:].bitcast(FP8X4),
+                            scales=w_scales[g][:],
+                            in_=w_bf[g][:].rearrange("p h n i -> p (h n i)"),
+                        )
                 for c in range(start // N_TILE, (start + width) // N_TILE):
                     multiply(a, c)
                     if a == PASSES - 1:

@@ -24,8 +24,7 @@ N_TILE = 512
 BANKS = S // N_TILE
 PER_COL = 16
 HI_MASK = -(1 << 20)
-SIGN_BIT = -(1 << 31)
-GATHER_WIDTHS = (2048, 1024, 512)
+HALF = S // 2
 OUT_WIDTHS = (512, 512, 512, 256, 128, 128)
 
 
@@ -38,71 +37,37 @@ def tile_list_tabts_silu_kernel(tc, tab_words, tab_scales, w, ts, b, offs, out):
 
         offsets = keep.tile([P, S // PER_COL], U16, name="offsets")
         scale_window = keep.tile([P, T // 4], I32, name="scale_window", tag="reused", align_bytes=64)
-        nc.vector.memset(scale_window[:], 0)
+        nc.vector.memset(scale_window[32:64, :], 0)
+        nc.vector.memset(scale_window[64:112, :], 0)
         planes = keep.tile([P, PASSES, S // 4], I32, name="planes", align_bytes=64)
-        nc.vector.memset(planes[:].rearrange("p a s -> p (a s)"), 0)
+        nc.gpsimd.memset(planes[:].rearrange("p a s -> p (a s)"), 0)
 
-        w_raw = [keep.tile([P, PACK, M], F32, name=f"w_raw{a}", align_bytes=64) for a in range(PASSES)]
-        for a in range(PASSES):
-            rows = w[a * K_PASS : (a + 1) * K_PASS, :]
-            nc.sync.dma_start(out=w_raw[a][:], in_=rows.rearrange("(p i) n -> p i n", i=PACK))
         nc.sync.dma_start(offsets[:], offs)
-        bias = keep.tile([P, 1], F32, name="bias")
-        nc.sync.dma_start(out=bias[:], in_=b.rearrange("(p o) -> p o", o=1))
         scale_rows = tab_scales.rearrange("a q t -> (a q) t").bitcast(I32)
         nc.sync.dma_start(out=scale_window[0:32, :], in_=scale_rows[0:32, :])
-        nc.sync.dma_start(out=scale_window[64:P:4, :], in_=scale_rows[32:48, :])
+        nc.sync.dma_start(out=scale_window[112:P, :], in_=scale_rows[32:48, :])
+        ts_rows = keep.tile([P, T // P], F32, name="ts_rows", tag="ts_then_w", align_bytes=64)
+        nc.sync.dma_start(out=ts_rows[:], in_=ts[0].rearrange("(p c) -> p c", p=P))
 
         def load_words(a, window):
             nc.sync.dma_start(out=window[:], in_=tab_words[a].rearrange("p t i -> p (t i)").bitcast(I32))
 
         word_window = [keep.tile([P, T], I32, name=f"word_window{a}", align_bytes=64) for a in range(PASSES - 1)]
         load_words(0, word_window[0])
-        ts_rows = keep.tile([P, T // P], F32, name="ts_rows", align_bytes=64)
-        nc.sync.dma_start(out=ts_rows[:], in_=ts[0].rearrange("(p c) -> p c", p=P))
+        w_all = keep.tile([P, PASSES, PACK, M], F32, name="w_all", align_bytes=64)
+        nc.sync.dma_start(
+            out=w_all[:].rearrange("p a i n -> p a (i n)"), in_=w.rearrange("(a p i) n -> p a (i n)", p=P, i=PACK)
+        )
+        w_raw = [w_all[:, a] for a in range(PASSES)]
         load_words(1, word_window[1])
+        bias = keep.tile([P, 1], F32, name="bias")
+        nc.sync.dma_start(out=bias[:], in_=b.rearrange("(p o) -> p o", o=1))
 
         identity = keep.tile([P, P], F32, name="identity", align_bytes=64)
         make_identity(nc, identity[:])
 
-        neg_hi = [keep.tile([P, PACK, M], I32, name=f"neg_hi{a}", align_bytes=64) for a in range(PASSES)]
-        lo_turned = [keep.tile([M, PACK, P], F32, name=f"lo_turned{a}", align_bytes=64) for a in range(PASSES)]
-        w_bf = [keep.tile([P, 2, M, PACK], BF16, name=f"w_bf{a}", align_bytes=64) for a in range(PASSES)]
-        w_codes = [keep.tile([P, 2 * M], U32, name=f"w_codes{a}", align_bytes=64) for a in range(PASSES)]
-        w_scales = [keep.tile([P, 2 * M], U8, name=f"w_scales{a}", align_bytes=64) for a in range(PASSES)]
-        for a in range(PASSES):
-            nc.vector.tensor_scalar(
-                out=neg_hi[a][:], in0=w_raw[a][:].bitcast(I32), scalar1=HI_MASK, scalar2=SIGN_BIT,
-                op0=ALU.bitwise_and, op1=ALU.bitwise_xor,
-            )
-        for a in range(PASSES):
-            neg = neg_hi[a][:].bitcast(F32)
-            bank = turn.tile([P, PACK, P], F32, name="bank")
-            for i in range(PACK):
-                nc.tensor.matmul(bank[:, i, :], w_raw[a][:, i, :], identity[:], start=True, stop=False, is_transpose=True)
-                nc.tensor.matmul(bank[:, i, :], neg[:, i, :], identity[:], start=False, stop=True, is_transpose=True)
-            nc.scalar.copy(out=lo_turned[a][:], in_=bank[:])
-            nc.scalar.activation(out=w_bf[a][:, 0], in_=neg.rearrange("p i n -> p n i"), func=ACT.Copy, scale=-1.0)
-        for a in range(PASSES):
-            bank = turn.tile([P, PACK, P], F32, name="bank")
-            for i in range(PACK):
-                nc.tensor.transpose(bank[:, i, :], lo_turned[a][:, i, :], identity[:])
-            nc.scalar.activation(out=w_bf[a][:, 1], in_=bank[:].rearrange("p i n -> p n i"), func=ACT.Copy)
-
         picked_rows = keep.tile([P, S], U8, name="picked_rows", align_bytes=64)
         nc.vector.tensor_copy(picked_rows[:], scale_window[:].bitcast(U8).indirect(offsets[:]))
-        last_window = keep.tile([P, T], I32, name="last_window", tag="reused", align_bytes=64)
-        word_window.append(last_window)
-        for a in range(PASSES):
-            first, step = ((0, 1), (16, 1), (64, 4))[a]
-            for r in range(4):
-                nc.sync.dma_start(
-                    out=planes[32 * r : 32 * r + 4, a, :],
-                    in_=picked_rows[first + 4 * step * r : first + 4 * step * (r + 1) : step, :].bitcast(I32),
-                )
-            if a == 0:
-                load_words(PASSES - 1, last_window)
-        picked_scales = planes[:].bitcast(U8)
 
         ts_window = keep.tile([P, T], F32, name="ts_window", align_bytes=64)
         ts_by_row = ts_window[:].rearrange("p (r c) -> p r c", r=P)
@@ -113,12 +78,32 @@ def tile_list_tabts_silu_kernel(tc, tab_words, tab_scales, w, ts, b, offs, out):
                 nc.tensor.transpose(bank[:, j, :], column.to_broadcast([P, P]), identity[:])
             nc.scalar.copy(out=ts_by_row[:, :, c0 : c0 + 4], in_=bank[:].rearrange("p j r -> p r j"))
 
-        picked = [keep.tile([P, S], U32, name=f"picked{a}", align_bytes=64) for a in range(PASSES)]
+        last_window = keep.tile([P, T], I32, name="last_window", tag="reused", align_bytes=64)
+        word_window.append(last_window)
+        for a in range(PASSES):
+            first = (0, 16, 112)[a]
+            for r in range(4):
+                nc.sync.dma_start(
+                    out=planes[32 * r : 32 * r + 4, a, :],
+                    in_=picked_rows[first + 4 * r : first + 4 * (r + 1), :].bitcast(I32),
+                )
+            if a == 0:
+                load_words(PASSES - 1, last_window)
+        picked_scales = planes[:].bitcast(U8)
+
         acc = [psum.tile([M, N_TILE], F32, name=f"acc{c}") for c in range(BANKS)]
         sums = keep.tile([M, S], F32, name="sums", align_bytes=64)
 
         def list_slice(start, width):
             return offsets[:, start // PER_COL : (start + width) // PER_COL]
+
+        picked = {}
+
+        def gather_words(a, start, width, tag):
+            tile = keep.tile([P, width], U32, name=f"picked{a}_{start}", tag=tag, align_bytes=64)
+            nc.vector.tensor_copy(tile[:], word_window[a][:].bitcast(U32).indirect(list_slice(start, width)))
+            for c in range(width // N_TILE):
+                picked[a, start // N_TILE + c] = tile[:, c * N_TILE : (c + 1) * N_TILE]
 
         def multiply(a, c):
             cols = slice(c * N_TILE, (c + 1) * N_TILE)
@@ -128,30 +113,47 @@ def tile_list_tabts_silu_kernel(tc, tab_words, tab_scales, w, ts, b, offs, out):
                     out=acc[c][:],
                     lhsT=w_codes[a][:, w_cols].bitcast(FP8X4),
                     lhsT_scale=w_scales[a][:, w_cols],
-                    rhs=picked[a][:, cols].bitcast(FP8X4),
+                    rhs=picked[a, c].bitcast(FP8X4),
                     rhs_scale=picked_scales[:, a, cols],
                     start=(a == 0 and h == 0),
                     stop=(a == PASSES - 1 and h == 1),
                 )
 
-        for a, width in enumerate(GATHER_WIDTHS):
-            for start in range(0, S, width):
-                nc.vector.tensor_copy(
-                    picked[a][:, start : start + width],
-                    word_window[a][:].bitcast(U32).indirect(list_slice(start, width)),
-                )
-                if a == 0:
-                    for g in range(PASSES):
-                        nc.vector.quantize_mx(
-                            out=w_codes[g][:].bitcast(FP8X4),
-                            scales=w_scales[g][:],
-                            in_=w_bf[g][:].rearrange("p h n i -> p (h n i)"),
-                        )
-                for c in range(start // N_TILE, (start + width) // N_TILE):
-                    multiply(a, c)
-                    if a == PASSES - 1:
-                        cols = slice(c * N_TILE, (c + 1) * N_TILE)
-                        nc.scalar.activation(out=sums[:, cols], in_=acc[c][:], func=ACT.Copy)
+        hi_mask = keep.tile([P, 1], I32, name="hi_mask", tag="mask_then_words", align_bytes=64)
+        nc.gpsimd.memset(hi_mask[:], HI_MASK)
+        gather_words(0, 0, HALF, "picked0")
+        w_hi = [keep.tile([P, PACK, M], I32, name=f"w_hi{a}", align_bytes=64) for a in range(PASSES)]
+        w_lo = [keep.tile([P, PACK, M], F32, name=f"w_lo{a}", align_bytes=64) for a in range(PASSES)]
+        w_bf = keep.tile([P, PASSES, 2, M, PACK], BF16, name="w_bf", tag="ts_then_w", align_bytes=64)
+        w_codes = [keep.tile([P, 2 * M], U32, name=f"w_codes{a}", align_bytes=64) for a in range(PASSES)]
+        w_scales = [keep.tile([P, 2 * M], U8, name=f"w_scales{a}", align_bytes=64) for a in range(PASSES)]
+        for a in range(PASSES):
+            nc.vector.tensor_scalar(
+                out=w_hi[a][:], in0=w_raw[a].bitcast(I32), scalar1=hi_mask[:], scalar2=None, op0=ALU.bitwise_and
+            )
+        for a in range(PASSES):
+            hi = w_hi[a][:].bitcast(F32)
+            nc.gpsimd.tensor_tensor(w_lo[a][:], w_raw[a], hi, ALU.subtract)
+            nc.scalar.activation(out=w_bf[:, a, 0], in_=hi.rearrange("p i n -> p n i"), func=ACT.Copy)
+            nc.scalar.activation(out=w_bf[:, a, 1], in_=w_lo[a][:].rearrange("p i n -> p n i"), func=ACT.Copy)
+
+        gather_words(0, HALF, HALF, "mask_then_words")
+        gather_words(1, 0, HALF, "picked1")
+        for g in range(PASSES):
+            nc.vector.quantize_mx(
+                out=w_codes[g][:].bitcast(FP8X4),
+                scales=w_scales[g][:],
+                in_=w_bf[:, g].rearrange("p h n i -> p (h n i)"),
+            )
+        gather_words(1, HALF, HALF, "ts_then_w")
+        for a in range(PASSES - 1):
+            for c in range(BANKS):
+                multiply(a, c)
+        for c in range(BANKS):
+            gather_words(PASSES - 1, c * N_TILE, N_TILE, f"picked2_{c}")
+            multiply(PASSES - 1, c)
+            cols = slice(c * N_TILE, (c + 1) * N_TILE)
+            nc.scalar.activation(out=sums[:, cols], in_=acc[c][:], func=ACT.Copy)
 
         scaled = keep.tile([M, S], F32, name="scaled", align_bytes=64)
         result = keep.tile([M, S], F32, name="result", align_bytes=64)

@@ -52,19 +52,20 @@ def tile_list_tabts_silu_kernel(tc, tab_words, tab_scales, w, ts, b, offs, out):
         def load_words(a, window):
             nc.sync.dma_start(out=window[:], in_=tab_words[a].rearrange("p t i -> p (t i)").bitcast(I32))
 
-        word_window = [keep.tile([P, T], I32, name=f"word_window{a}", align_bytes=64) for a in range(PASSES - 1)]
+        word_window = [keep.tile([P, T], I32, name=f"word_window{a}", tag=f"word_window{a}", align_bytes=64) for a in range(PASSES - 1)]
         load_words(0, word_window[0])
         w_all = keep.tile([P, PASSES, PACK, M], F32, name="w_all", align_bytes=64)
         nc.sync.dma_start(
             out=w_all[:].rearrange("p a i n -> p a (i n)"), in_=w.rearrange("(a p i) n -> p a (i n)", p=P, i=PACK)
         )
-        w_raw = [w_all[:, a] for a in range(PASSES)]
         load_words(1, word_window[1])
         bias = keep.tile([P, 1], F32, name="bias")
         nc.sync.dma_start(out=bias[:], in_=b.rearrange("(p o) -> p o", o=1))
 
         identity = keep.tile([P, P], F32, name="identity", align_bytes=64)
         make_identity(nc, identity[:])
+        warm = keep.tile([P, 1], F32, name="warm")
+        nc.scalar.activation(out=warm[:], in_=identity[:, 0:1], func=ACT.Silu)
 
         picked_rows = keep.tile([P, S], U8, name="picked_rows", align_bytes=64)
         nc.vector.tensor_copy(picked_rows[:], scale_window[:].bitcast(U8).indirect(offsets[:]))
@@ -122,30 +123,41 @@ def tile_list_tabts_silu_kernel(tc, tab_words, tab_scales, w, ts, b, offs, out):
         hi_mask = keep.tile([P, 1], I32, name="hi_mask", tag="mask_then_words", align_bytes=64)
         nc.gpsimd.memset(hi_mask[:], HI_MASK)
         gather_words(0, 0, HALF, "picked0")
-        w_hi = [keep.tile([P, PACK, M], I32, name=f"w_hi{a}", align_bytes=64) for a in range(PASSES)]
-        w_lo = [keep.tile([P, PACK, M], F32, name=f"w_lo{a}", align_bytes=64) for a in range(PASSES)]
-        w_bf = keep.tile([P, PASSES, 2, M, PACK], BF16, name="w_bf", tag="ts_then_w", align_bytes=64)
-        w_codes = [keep.tile([P, 2 * M], U32, name=f"w_codes{a}", align_bytes=64) for a in range(PASSES)]
-        w_scales = [keep.tile([P, 2 * M], U8, name=f"w_scales{a}", align_bytes=64) for a in range(PASSES)]
-        for a in range(PASSES):
-            nc.vector.tensor_scalar(
-                out=w_hi[a][:], in0=w_raw[a].bitcast(I32), scalar1=hi_mask[:], scalar2=None, op0=ALU.bitwise_and
-            )
-        for a in range(PASSES):
-            hi = w_hi[a][:].bitcast(F32)
-            nc.gpsimd.tensor_tensor(w_lo[a][:], w_raw[a], hi, ALU.subtract)
-            nc.scalar.activation(out=w_bf[:, a, 0], in_=hi.rearrange("p i n -> p n i"), func=ACT.Copy)
-            nc.scalar.activation(out=w_bf[:, a, 1], in_=w_lo[a][:].rearrange("p i n -> p n i"), func=ACT.Copy)
+        w_hi = keep.tile([P, PASSES, PACK, M], I32, name="w_hi", align_bytes=64)
+        nc.vector.tensor_scalar(
+            out=w_hi[:], in0=w_all[:].bitcast(I32), scalar1=hi_mask[:], scalar2=None, op0=ALU.bitwise_and
+        )
+        w_codes, w_scales = {}, {}
 
-        gather_words(0, HALF, HALF, "mask_then_words")
-        gather_words(1, 0, HALF, "picked1")
-        for g in range(PASSES):
+        def round_parts(passes, lo_tag, rounded_tag):
+            n = len(passes)
+            lo = keep.tile([P, n, PACK, M], F32, name=f"w_lo{passes[0]}", tag=lo_tag, align_bytes=64)
+            rounded = keep.tile([P, n, 2, M, PACK], BF16, name=f"w_bf{passes[0]}", tag=rounded_tag, align_bytes=64)
+            for j, a in enumerate(passes):
+                hi = w_hi[:, a].bitcast(F32)
+                nc.gpsimd.tensor_tensor(lo[:, j], w_all[:, a], hi, ALU.subtract)
+                nc.scalar.activation(out=rounded[:, j, 0], in_=hi.rearrange("p i n -> p n i"), func=ACT.Copy)
+                nc.scalar.activation(out=rounded[:, j, 1], in_=lo[:, j].rearrange("p i n -> p n i"), func=ACT.Copy)
+            return rounded
+
+        def quantize_parts(passes, rounded, codes_tag):
+            n = len(passes)
+            codes = keep.tile([P, n, 2 * M], U32, name=f"w_codes{passes[0]}", tag=codes_tag, align_bytes=64)
+            scales = keep.tile([P, n, 2 * M], U8, name=f"w_scales{passes[0]}", align_bytes=64)
             nc.vector.quantize_mx(
-                out=w_codes[g][:].bitcast(FP8X4),
-                scales=w_scales[g][:],
-                in_=w_bf[:, g].rearrange("p h n i -> p (h n i)"),
+                out=codes[:].rearrange("p a c -> p (a c)").bitcast(FP8X4),
+                scales=scales[:].rearrange("p a c -> p (a c)"),
+                in_=rounded[:].rearrange("p a h n i -> p (a h n i)"),
             )
-        gather_words(1, HALF, HALF, "ts_then_w")
+            for j, a in enumerate(passes):
+                w_codes[a], w_scales[a] = codes[:, j], scales[:, j]
+
+        rounded = round_parts([0], "w_lo0", "ts_then_w")
+        gather_words(0, HALF, HALF, "mask_then_words")
+        quantize_parts([0], rounded, "w_codes0")
+        rounded = round_parts([1, 2], "ts_then_w", "w_bf1")
+        gather_words(1, 0, S, "picked1")
+        quantize_parts([1, 2], rounded, "word_window1")
         for a in range(PASSES - 1):
             for c in range(BANKS):
                 multiply(a, c)

@@ -23,8 +23,8 @@ PASSES = K // K_PASS
 N_TILE = 512
 BANKS = S // N_TILE
 PER_COL = 16
-HI_MASK = -(1 << 20)
-HALF = S // 2
+PAIR_MASK = -0x000F0010
+FIRST = 1024
 OUT_WIDTHS = (512, 512, 512, 256, 128, 128)
 
 
@@ -39,13 +39,11 @@ def tile_list_tabts_silu_kernel(tc, tab_words, tab_scales, w, ts, b, offs, out):
         scale_window = keep.tile([P, T // 4], I32, name="scale_window", tag="reused", align_bytes=64)
         nc.vector.memset(scale_window[32:64, :], 0)
         nc.vector.memset(scale_window[64:112, :], 0)
-        planes = keep.tile([P, PASSES, S // 4], I32, name="planes", align_bytes=64)
-        nc.gpsimd.memset(planes[:].rearrange("p a s -> p (a s)"), 0)
 
-        nc.sync.dma_start(offsets[:], offs)
         scale_rows = tab_scales.rearrange("a q t -> (a q) t").bitcast(I32)
         nc.sync.dma_start(out=scale_window[0:32, :], in_=scale_rows[0:32, :])
         nc.sync.dma_start(out=scale_window[112:P, :], in_=scale_rows[32:48, :])
+        nc.sync.dma_start(offsets[:], offs)
         ts_rows = keep.tile([P, T // P], F32, name="ts_rows", tag="ts_then_w", align_bytes=64)
         nc.sync.dma_start(out=ts_rows[:], in_=ts[0].rearrange("(p c) -> p c", p=P))
 
@@ -55,17 +53,19 @@ def tile_list_tabts_silu_kernel(tc, tab_words, tab_scales, w, ts, b, offs, out):
         word_window = [keep.tile([P, T], I32, name=f"word_window{a}", tag=f"word_window{a}", align_bytes=64) for a in range(PASSES - 1)]
         load_words(0, word_window[0])
         w_all = keep.tile([P, PASSES, PACK, M], F32, name="w_all", align_bytes=64)
-        nc.sync.dma_start(
-            out=w_all[:].rearrange("p a i n -> p a (i n)"), in_=w.rearrange("(a p i) n -> p a (i n)", p=P, i=PACK)
-        )
+        w_rows = w.rearrange("(a p i) n -> p a (i n)", p=P, i=PACK)
+        for lo, hi in ((0, 1), (1, PASSES)):
+            nc.sync.dma_start(out=w_all[:, lo:hi].rearrange("p a i n -> p a (i n)"), in_=w_rows[:, lo:hi])
         load_words(1, word_window[1])
         bias = keep.tile([P, 1], F32, name="bias")
         nc.sync.dma_start(out=bias[:], in_=b.rearrange("(p o) -> p o", o=1))
 
         identity = keep.tile([P, P], F32, name="identity", align_bytes=64)
         make_identity(nc, identity[:])
-        warm = keep.tile([P, 1], F32, name="warm")
+        warm = keep.tile([P, 1], F32, name="warm", tag="planes", align_bytes=64)
         nc.scalar.activation(out=warm[:], in_=identity[:, 0:1], func=ACT.Silu)
+        planes = keep.tile([P, PASSES, S // 4], I32, name="planes", tag="planes", align_bytes=64)
+        nc.gpsimd.memset(planes[:].rearrange("p a s -> p (a s)"), 0)
 
         picked_rows = keep.tile([P, S], U8, name="picked_rows", align_bytes=64)
         nc.vector.tensor_copy(picked_rows[:], scale_window[:].bitcast(U8).indirect(offsets[:]))
@@ -109,60 +109,68 @@ def tile_list_tabts_silu_kernel(tc, tab_words, tab_scales, w, ts, b, offs, out):
         def multiply(a, c):
             cols = slice(c * N_TILE, (c + 1) * N_TILE)
             for h in range(2):
-                w_cols = slice(h * M, (h + 1) * M)
                 nc.tensor.matmul_mx(
                     out=acc[c][:],
-                    lhsT=w_codes[a][:, w_cols].bitcast(FP8X4),
-                    lhsT_scale=w_scales[a][:, w_cols],
+                    lhsT=w_codes[a, h].bitcast(FP8X4),
+                    lhsT_scale=w_scales[a, h],
                     rhs=picked[a, c].bitcast(FP8X4),
                     rhs_scale=picked_scales[:, a, cols],
                     start=(a == 0 and h == 0),
                     stop=(a == PASSES - 1 and h == 1),
                 )
 
-        hi_mask = keep.tile([P, 1], I32, name="hi_mask", tag="mask_then_words", align_bytes=64)
-        nc.gpsimd.memset(hi_mask[:], HI_MASK)
-        gather_words(0, 0, HALF, "picked0")
-        w_hi = keep.tile([P, PASSES, PACK, M], I32, name="w_hi", align_bytes=64)
-        nc.vector.tensor_scalar(
-            out=w_hi[:], in0=w_all[:].bitcast(I32), scalar1=hi_mask[:], scalar2=None, op0=ALU.bitwise_and
-        )
         w_codes, w_scales = {}, {}
 
-        def round_parts(passes, lo_tag, rounded_tag):
+        def quantize_parts(passes, rounded):
             n = len(passes)
-            lo = keep.tile([P, n, PACK, M], F32, name=f"w_lo{passes[0]}", tag=lo_tag, align_bytes=64)
-            rounded = keep.tile([P, n, 2, M, PACK], BF16, name=f"w_bf{passes[0]}", tag=rounded_tag, align_bytes=64)
-            for j, a in enumerate(passes):
-                hi = w_hi[:, a].bitcast(F32)
-                nc.gpsimd.tensor_tensor(lo[:, j], w_all[:, a], hi, ALU.subtract)
-                nc.scalar.activation(out=rounded[:, j, 0], in_=hi.rearrange("p i n -> p n i"), func=ACT.Copy)
-                nc.scalar.activation(out=rounded[:, j, 1], in_=lo[:, j].rearrange("p i n -> p n i"), func=ACT.Copy)
-            return rounded
-
-        def quantize_parts(passes, rounded, codes_tag):
-            n = len(passes)
-            codes = keep.tile([P, n, 2 * M], U32, name=f"w_codes{passes[0]}", tag=codes_tag, align_bytes=64)
-            scales = keep.tile([P, n, 2 * M], U8, name=f"w_scales{passes[0]}", align_bytes=64)
+            codes = keep.tile([P, 2, n, M], U32, name=f"w_codes{passes[0]}", align_bytes=64)
+            scales = keep.tile([P, 2, n, M], U8, name=f"w_scales{passes[0]}", align_bytes=64)
             nc.vector.quantize_mx(
-                out=codes[:].rearrange("p a c -> p (a c)").bitcast(FP8X4),
-                scales=scales[:].rearrange("p a c -> p (a c)"),
-                in_=rounded[:].rearrange("p a h n i -> p (a h n i)"),
+                out=codes[:].rearrange("p h a c -> p (h a c)").bitcast(FP8X4),
+                scales=scales[:].rearrange("p h a c -> p (h a c)"),
+                in_=rounded[:].rearrange("p h a n i -> p (h a n i)"),
             )
             for j, a in enumerate(passes):
-                w_codes[a], w_scales[a] = codes[:, j], scales[:, j]
+                for h in range(2):
+                    w_codes[a, h], w_scales[a, h] = codes[:, h, j], scales[:, h, j]
 
-        rounded = round_parts([0], "w_lo0", "ts_then_w")
-        gather_words(0, HALF, HALF, "mask_then_words")
-        quantize_parts([0], rounded, "w_codes0")
-        rounded = round_parts([1, 2], "ts_then_w", "w_bf1")
+        def as_words(ap):
+            return ap.rearrange("p a n i -> p (a n i)").bitcast(I32)
+
+        gather_words(0, 0, FIRST, "picked0")
+        one = keep.tile([P, 1], F32, name="one", tag="one_then_words", align_bytes=64)
+        nc.gpsimd.memset(one[:], 1.0)
+        upper = keep.tile([P, PASSES, M, PACK], BF16, name="upper", align_bytes=64)
+        for a in range(PASSES):
+            halves = w_all[:, a].bitcast(BF16).rearrange("p i (n t) -> p n i t", t=2)
+            scale = one[:] if a == 0 else 1.0
+            nc.scalar.activation(out=upper[:, a], in_=halves[:, :, :, 1], func=ACT.Copy, scale=scale)
+        first_bf = keep.tile([P, 2, 1, M, PACK], BF16, name="first_bf", tag="ts_then_w", align_bytes=64)
+        rest_bf = keep.tile([P, 2, 2, M, PACK], BF16, name="rest_bf", align_bytes=64)
+
+        def mask(rounded, lo, hi):
+            nc.vector.tensor_scalar(
+                out=as_words(rounded[:, 0]), in0=as_words(upper[:, lo:hi]), scalar1=PAIR_MASK, scalar2=None,
+                op0=ALU.bitwise_and,
+            )
+
+        mask(first_bf, 0, 1)
+        nc.gpsimd.tensor_tensor(first_bf[:, 1, 0], w_all[:, 0].rearrange("p i n -> p n i"), first_bf[:, 0, 0], ALU.subtract)
+        gather_words(0, FIRST, S - FIRST, "one_then_words")
+        mask(rest_bf, 1, PASSES)
+        quantize_parts([0], first_bf)
+        rest_lo = keep.tile([P, 2, M, PACK], F32, name="rest_lo", tag="ts_then_w", align_bytes=64)
+        for j in range(2):
+            nc.gpsimd.tensor_tensor(rest_lo[:, j], w_all[:, 1 + j].rearrange("p i n -> p n i"), rest_bf[:, 0, j], ALU.subtract)
+            nc.scalar.copy(out=rest_bf[:, 1, j], in_=rest_lo[:, j])
         gather_words(1, 0, S, "picked1")
-        quantize_parts([1, 2], rounded, "word_window1")
+        quantize_parts([1, 2], rest_bf)
         for a in range(PASSES - 1):
             for c in range(BANKS):
                 multiply(a, c)
         for c in range(BANKS):
-            gather_words(PASSES - 1, c * N_TILE, N_TILE, f"picked2_{c}")
+            if c % 2 == 0:
+                gather_words(PASSES - 1, c * N_TILE, 2 * N_TILE, f"picked2_{c}")
             multiply(PASSES - 1, c)
             cols = slice(c * N_TILE, (c + 1) * N_TILE)
             nc.scalar.activation(out=sums[:, cols], in_=acc[c][:], func=ACT.Copy)

@@ -18,13 +18,16 @@ ACT = mybir.ActivationFunctionType
 
 P = 128
 PACK = 4
-K_PASS = P * PACK
-PASSES = K // K_PASS
+PASSES = K // (P * PACK)
 N_TILE = 512
 BANKS = S // N_TILE
+HALF = S // 2
 PER_COL = 16
+QUADRANT = 32
+ROWS = 4
+TURNS = 4
 PAIR_MASK = -0x000F0010
-FIRST = 1024
+FIRST_ROW = (0, 16, 112)
 OUT_WIDTHS = (512, 512, 512, 256, 128, 128)
 
 
@@ -36,35 +39,37 @@ def tile_list_tabts_silu_kernel(tc, tab_words, tab_scales, w, ts, b, offs, out):
         turn = ctx.enter_context(tc.psum_pool(name="turn", bufs=4))
 
         offsets = keep.tile([P, S // PER_COL], U16, name="offsets")
-        scale_window = keep.tile([P, T // 4], I32, name="scale_window", tag="reused", align_bytes=64)
-        nc.vector.memset(scale_window[32:64, :], 0)
-        nc.vector.memset(scale_window[64:112, :], 0)
+        scale_window = keep.tile([P, T // 4], I32, name="scale_window", tag="scales_then_words", align_bytes=64)
+        nc.vector.memset(scale_window[QUADRANT : 2 * QUADRANT, :], 0)
+        nc.vector.memset(scale_window[2 * QUADRANT : FIRST_ROW[2], :], 0)
 
         scale_rows = tab_scales.rearrange("a q t -> (a q) t").bitcast(I32)
-        nc.sync.dma_start(out=scale_window[0:32, :], in_=scale_rows[0:32, :])
-        nc.sync.dma_start(out=scale_window[112:P, :], in_=scale_rows[32:48, :])
+        nc.sync.dma_start(out=scale_window[0:QUADRANT, :], in_=scale_rows[0:QUADRANT, :])
+        nc.sync.dma_start(out=scale_window[FIRST_ROW[2] :, :], in_=scale_rows[QUADRANT:, :])
         nc.sync.dma_start(offsets[:], offs)
-        ts_rows = keep.tile([P, T // P], F32, name="ts_rows", tag="ts_then_w", align_bytes=64)
+        ts_rows = keep.tile([P, T // P], F32, name="ts_rows", tag="ts_then_weights", align_bytes=64)
         nc.sync.dma_start(out=ts_rows[:], in_=ts[0].rearrange("(p c) -> p c", p=P))
 
         def load_words(a, window):
             nc.sync.dma_start(out=window[:], in_=tab_words[a].rearrange("p t i -> p (t i)").bitcast(I32))
 
-        word_window = [keep.tile([P, T], I32, name=f"word_window{a}", tag=f"word_window{a}", align_bytes=64) for a in range(PASSES - 1)]
+        word_window = [keep.tile([P, T], I32, name=f"word_window{a}", align_bytes=64) for a in range(PASSES - 1)]
         load_words(0, word_window[0])
-        w_all = keep.tile([P, PASSES, PACK, M], F32, name="w_all", align_bytes=64)
         w_rows = w.rearrange("(a p i) n -> p a (i n)", p=P, i=PACK)
-        for lo, hi in ((0, 1), (1, PASSES)):
-            nc.sync.dma_start(out=w_all[:, lo:hi].rearrange("p a i n -> p a (i n)"), in_=w_rows[:, lo:hi])
+        w_first = keep.tile([P, PACK, M], F32, name="w_first", tag="w_then_words", align_bytes=64)
+        nc.sync.dma_start(out=w_first[:].rearrange("p i n -> p (i n)"), in_=w_rows[:, 0])
+        w_rest = keep.tile([P, PASSES - 1, PACK, M], F32, name="w_rest", align_bytes=64)
+        nc.sync.dma_start(out=w_rest[:].rearrange("p a i n -> p a (i n)"), in_=w_rows[:, 1:])
+        w_raw = [w_first[:], w_rest[:, 0], w_rest[:, 1]]
         load_words(1, word_window[1])
         bias = keep.tile([P, 1], F32, name="bias")
         nc.sync.dma_start(out=bias[:], in_=b.rearrange("(p o) -> p o", o=1))
 
         identity = keep.tile([P, P], F32, name="identity", align_bytes=64)
         make_identity(nc, identity[:])
-        warm = keep.tile([P, 1], F32, name="warm", tag="planes", align_bytes=64)
+        warm = keep.tile([P, 1], F32, name="warm", tag="warm_then_planes", align_bytes=64)
         nc.scalar.activation(out=warm[:], in_=identity[:, 0:1], func=ACT.Silu)
-        planes = keep.tile([P, PASSES, S // 4], I32, name="planes", tag="planes", align_bytes=64)
+        planes = keep.tile([P, PASSES, S // 4], I32, name="planes", tag="warm_then_planes", align_bytes=64)
         nc.gpsimd.memset(planes[:].rearrange("p a s -> p (a s)"), 0)
 
         picked_rows = keep.tile([P, S], U8, name="picked_rows", align_bytes=64)
@@ -72,21 +77,21 @@ def tile_list_tabts_silu_kernel(tc, tab_words, tab_scales, w, ts, b, offs, out):
 
         ts_window = keep.tile([P, T], F32, name="ts_window", align_bytes=64)
         ts_by_row = ts_window[:].rearrange("p (r c) -> p r c", r=P)
-        for c0 in range(0, T // P, 4):
-            bank = turn.tile([P, 4, P], F32, name="bank")
-            for j in range(4):
+        for c0 in range(0, T // P, TURNS):
+            bank = turn.tile([P, TURNS, P], F32, name="bank")
+            for j in range(TURNS):
                 column = ts_rows[:, c0 + j : c0 + j + 1]
                 nc.tensor.transpose(bank[:, j, :], column.to_broadcast([P, P]), identity[:])
-            nc.scalar.copy(out=ts_by_row[:, :, c0 : c0 + 4], in_=bank[:].rearrange("p j r -> p r j"))
+            nc.scalar.copy(out=ts_by_row[:, :, c0 : c0 + TURNS], in_=bank[:].rearrange("p j r -> p r j"))
 
-        last_window = keep.tile([P, T], I32, name="last_window", tag="reused", align_bytes=64)
+        last_window = keep.tile([P, T], I32, name="last_window", tag="scales_then_words", align_bytes=64)
         word_window.append(last_window)
         for a in range(PASSES):
-            first = (0, 16, 112)[a]
-            for r in range(4):
+            for quad in range(P // QUADRANT):
+                row = FIRST_ROW[a] + ROWS * quad
                 nc.sync.dma_start(
-                    out=planes[32 * r : 32 * r + 4, a, :],
-                    in_=picked_rows[first + 4 * r : first + 4 * (r + 1), :].bitcast(I32),
+                    out=planes[QUADRANT * quad : QUADRANT * quad + ROWS, a, :],
+                    in_=picked_rows[row : row + ROWS, :].bitcast(I32),
                 )
             if a == 0:
                 load_words(PASSES - 1, last_window)
@@ -106,71 +111,79 @@ def tile_list_tabts_silu_kernel(tc, tab_words, tab_scales, w, ts, b, offs, out):
             for c in range(width // N_TILE):
                 picked[a, start // N_TILE + c] = tile[:, c * N_TILE : (c + 1) * N_TILE]
 
-        def multiply(a, c):
-            cols = slice(c * N_TILE, (c + 1) * N_TILE)
-            for h in range(2):
-                nc.tensor.matmul_mx(
-                    out=acc[c][:],
-                    lhsT=w_codes[a, h].bitcast(FP8X4),
-                    lhsT_scale=w_scales[a, h],
-                    rhs=picked[a, c].bitcast(FP8X4),
-                    rhs_scale=picked_scales[:, a, cols],
-                    start=(a == 0 and h == 0),
-                    stop=(a == PASSES - 1 and h == 1),
-                )
-
         w_codes, w_scales = {}, {}
 
-        def quantize_parts(passes, rounded):
-            n = len(passes)
-            codes = keep.tile([P, 2, n, M], U32, name=f"w_codes{passes[0]}", align_bytes=64)
-            scales = keep.tile([P, 2, n, M], U8, name=f"w_scales{passes[0]}", align_bytes=64)
+        def multiply(a, c):
+            cols = slice(c * N_TILE, (c + 1) * N_TILE)
+            for part in range(2):
+                nc.tensor.matmul_mx(
+                    out=acc[c][:],
+                    lhsT=w_codes[a, part].bitcast(FP8X4),
+                    lhsT_scale=w_scales[a, part],
+                    rhs=picked[a, c].bitcast(FP8X4),
+                    rhs_scale=picked_scales[:, a, cols],
+                    start=(a == 0 and part == 0),
+                    stop=(a == PASSES - 1 and part == 1),
+                )
+
+        def quantize_parts(passes, rounded, tag):
+            count = len(passes)
+            codes = keep.tile([P, 2, count, M], U32, name=f"w_codes{passes[0]}", tag=tag, align_bytes=64)
+            scales = keep.tile([P, 2, count, M], U8, name=f"w_scales{passes[0]}", align_bytes=64)
             nc.vector.quantize_mx(
-                out=codes[:].rearrange("p h a c -> p (h a c)").bitcast(FP8X4),
-                scales=scales[:].rearrange("p h a c -> p (h a c)"),
+                out=codes[:].rearrange("p h a n -> p (h a n)").bitcast(FP8X4),
+                scales=scales[:].rearrange("p h a n -> p (h a n)"),
                 in_=rounded[:].rearrange("p h a n i -> p (h a n i)"),
             )
             for j, a in enumerate(passes):
-                for h in range(2):
-                    w_codes[a, h], w_scales[a, h] = codes[:, h, j], scales[:, h, j]
+                for part in range(2):
+                    w_codes[a, part], w_scales[a, part] = codes[:, part, j], scales[:, part, j]
 
-        def as_words(ap):
-            return ap.rearrange("p a n i -> p (a n i)").bitcast(I32)
+        def as_words(pairs):
+            return pairs.rearrange("p a n i -> p (a n i)").bitcast(I32)
 
-        gather_words(0, 0, FIRST, "picked0")
-        one = keep.tile([P, 1], F32, name="one", tag="one_then_words", align_bytes=64)
-        nc.gpsimd.memset(one[:], 1.0)
+        gather_words(0, 0, HALF, "words_then_codes")
+
+        w_woven = keep.tile([P, M, PACK], F32, name="w_woven", align_bytes=64)
         upper = keep.tile([P, PASSES, M, PACK], BF16, name="upper", align_bytes=64)
         for a in range(PASSES):
-            halves = w_all[:, a].bitcast(BF16).rearrange("p i (n t) -> p n i t", t=2)
-            scale = one[:] if a == 0 else 1.0
-            nc.scalar.activation(out=upper[:, a], in_=halves[:, :, :, 1], func=ACT.Copy, scale=scale)
-        first_bf = keep.tile([P, 2, 1, M, PACK], BF16, name="first_bf", tag="ts_then_w", align_bytes=64)
-        rest_bf = keep.tile([P, 2, 2, M, PACK], BF16, name="rest_bf", align_bytes=64)
+            halves = w_raw[a].bitcast(BF16).rearrange("p i (n t) -> p n i t", t=2)
+            nc.scalar.copy(out=upper[:, a], in_=halves[:, :, :, 1])
+            if a == 0:
+                nc.scalar.copy(out=w_woven[:], in_=w_raw[0].rearrange("p i n -> p n i"))
+        first_bf = keep.tile([P, 2, 1, M, PACK], BF16, name="first_bf", tag="ts_then_weights", align_bytes=64)
+        rest_bf = keep.tile([P, 2, PASSES - 1, M, PACK], BF16, name="rest_bf", align_bytes=64)
 
-        def mask(rounded, lo, hi):
+        def cut_to_hi(rounded, first, last):
             nc.vector.tensor_scalar(
-                out=as_words(rounded[:, 0]), in0=as_words(upper[:, lo:hi]), scalar1=PAIR_MASK, scalar2=None,
+                out=as_words(rounded[:, 0]),
+                in0=as_words(upper[:, first:last]),
+                scalar1=PAIR_MASK,
+                scalar2=None,
                 op0=ALU.bitwise_and,
             )
 
-        mask(first_bf, 0, 1)
-        nc.gpsimd.tensor_tensor(first_bf[:, 1, 0], w_all[:, 0].rearrange("p i n -> p n i"), first_bf[:, 0, 0], ALU.subtract)
-        gather_words(0, FIRST, S - FIRST, "one_then_words")
-        mask(rest_bf, 1, PASSES)
-        quantize_parts([0], first_bf)
-        rest_lo = keep.tile([P, 2, M, PACK], F32, name="rest_lo", tag="ts_then_w", align_bytes=64)
-        for j in range(2):
-            nc.gpsimd.tensor_tensor(rest_lo[:, j], w_all[:, 1 + j].rearrange("p i n -> p n i"), rest_bf[:, 0, j], ALU.subtract)
+        cut_to_hi(first_bf, 0, 1)
+        nc.gpsimd.tensor_tensor(first_bf[:, 1, 0], w_woven[:], first_bf[:, 0, 0], ALU.subtract)
+        gather_words(0, HALF, HALF, "w_then_words")
+        cut_to_hi(rest_bf, 1, PASSES)
+        quantize_parts([0], first_bf, "first_codes")
+
+        rest_lo = keep.tile([P, PASSES - 1, M, PACK], F32, name="rest_lo", tag="ts_then_weights", align_bytes=64)
+        for j in range(PASSES - 1):
+            w_by_column = w_raw[1 + j].rearrange("p i n -> p n i")
+            nc.gpsimd.tensor_tensor(rest_lo[:, j], w_by_column, rest_bf[:, 0, j], ALU.subtract)
             nc.scalar.copy(out=rest_bf[:, 1, j], in_=rest_lo[:, j])
         gather_words(1, 0, S, "picked1")
-        quantize_parts([1, 2], rest_bf)
-        for a in range(PASSES - 1):
-            for c in range(BANKS):
-                multiply(a, c)
         for c in range(BANKS):
-            if c % 2 == 0:
-                gather_words(PASSES - 1, c * N_TILE, 2 * N_TILE, f"picked2_{c}")
+            multiply(0, c)
+        quantize_parts([1, 2], rest_bf, "words_then_codes")
+        for c in range(BANKS):
+            multiply(1, c)
+
+        for c in range(BANKS):
+            if c * N_TILE % HALF == 0:
+                gather_words(PASSES - 1, c * N_TILE, HALF, f"picked2_{c}")
             multiply(PASSES - 1, c)
             cols = slice(c * N_TILE, (c + 1) * N_TILE)
             nc.scalar.activation(out=sums[:, cols], in_=acc[c][:], func=ACT.Copy)

@@ -28,7 +28,7 @@ ROWS = 4
 TURNS = 4
 PAIR_MASK = -0x000F0010
 FIRST_ROW = (0, 16, 112)
-OUT_WIDTHS = (512, 512, 512, 256, 128, 128)
+OUT_WIDTHS = (512, 512, 512, 320, 192)
 
 
 def tile_list_tabts_silu_kernel(tc, tab_words, tab_scales, w, ts, b, offs, out):
@@ -151,6 +151,9 @@ def tile_list_tabts_silu_kernel(tc, tab_words, tab_scales, w, ts, b, offs, out):
             nc.scalar.copy(out=upper[:, a], in_=halves[:, :, :, 1])
             if a == 0:
                 nc.scalar.copy(out=w_woven[:], in_=w_raw[0].rearrange("p i n -> p n i"))
+        rest_woven = keep.tile([P, PASSES - 1, M, PACK], F32, name="rest_woven", align_bytes=64)
+        for j in range(PASSES - 1):
+            nc.scalar.copy(out=rest_woven[:, j], in_=w_raw[1 + j].rearrange("p i n -> p n i"))
         first_bf = keep.tile([P, 2, 1, M, PACK], BF16, name="first_bf", tag="ts_then_weights", align_bytes=64)
         rest_bf = keep.tile([P, 2, PASSES - 1, M, PACK], BF16, name="rest_bf", align_bytes=64)
 
@@ -169,24 +172,21 @@ def tile_list_tabts_silu_kernel(tc, tab_words, tab_scales, w, ts, b, offs, out):
         cut_to_hi(rest_bf, 1, PASSES)
         quantize_parts([0], first_bf, "first_codes")
 
-        rest_lo = keep.tile([P, PASSES - 1, M, PACK], F32, name="rest_lo", tag="ts_then_weights", align_bytes=64)
-        for j in range(PASSES - 1):
-            w_by_column = w_raw[1 + j].rearrange("p i n -> p n i")
-            nc.gpsimd.tensor_tensor(rest_lo[:, j], w_by_column, rest_bf[:, 0, j], ALU.subtract)
-            nc.scalar.copy(out=rest_bf[:, 1, j], in_=rest_lo[:, j])
+        nc.gpsimd.tensor_tensor(rest_bf[:, 1], rest_woven[:], rest_bf[:, 0], ALU.subtract)
         gather_words(1, 0, S, "picked1")
         for c in range(BANKS):
             multiply(0, c)
         quantize_parts([1, 2], rest_bf, "words_then_codes")
-        for c in range(BANKS):
-            multiply(1, c)
 
-        for c in range(BANKS):
-            if c * N_TILE % HALF == 0:
-                gather_words(PASSES - 1, c * N_TILE, HALF, f"picked2_{c}")
-            multiply(PASSES - 1, c)
-            cols = slice(c * N_TILE, (c + 1) * N_TILE)
-            nc.scalar.activation(out=sums[:, cols], in_=acc[c][:], func=ACT.Copy)
+        for start in range(0, S, HALF):
+            gather_words(PASSES - 1, start, HALF, f"picked2_{start}")
+            banks = range(start // N_TILE, (start + HALF) // N_TILE)
+            for c in banks:
+                multiply(1, c)
+            for c in banks:
+                multiply(PASSES - 1, c)
+                cols = slice(c * N_TILE, (c + 1) * N_TILE)
+                nc.scalar.activation(out=sums[:, cols], in_=acc[c][:], func=ACT.Copy)
 
         scaled = keep.tile([M, S], F32, name="scaled", align_bytes=64)
         result = keep.tile([M, S], F32, name="result", align_bytes=64)

@@ -58,12 +58,12 @@ def tile_list_tabts_silu_kernel(tc, tab_words, tab_scales, w, ts, b, offs, out):
         w_rows = w.rearrange("(a p i) n -> p a (i n)", p=P, i=PACK)
         w_first = keep.tile([P, PACK, M], F32, name="w_first", tag="w_then_words", align_bytes=64)
         nc.sync.dma_start(out=w_first[:].rearrange("p i n -> p (i n)"), in_=w_rows[:, 0])
-        w_rest = keep.tile([P, PASSES - 1, PACK, M], F32, name="w_rest", align_bytes=64)
-        nc.sync.dma_start(out=w_rest[:].rearrange("p a i n -> p a (i n)"), in_=w_rows[:, 1:])
-        w_raw = [w_first[:], w_rest[:, 0], w_rest[:, 1]]
+        w_second = keep.tile([P, PACK, M], F32, name="w_second", align_bytes=64)
+        nc.sync.dma_start(out=w_second[:].rearrange("p i n -> p (i n)"), in_=w_rows[:, 1])
         load_words(1, word_window[1])
-        bias = keep.tile([P, 1], F32, name="bias")
-        nc.sync.dma_start(out=bias[:], in_=b.rearrange("(p o) -> p o", o=1))
+        w_third = keep.tile([P, PACK, M], F32, name="w_third", tag="w_then_words1", align_bytes=64)
+        nc.sync.dma_start(out=w_third[:].rearrange("p i n -> p (i n)"), in_=w_rows[:, 2])
+        w_raw = [w_first[:], w_second[:], w_third[:]]
 
         identity = keep.tile([P, P], F32, name="identity", align_bytes=64)
         make_identity(nc, identity[:])
@@ -96,6 +96,8 @@ def tile_list_tabts_silu_kernel(tc, tab_words, tab_scales, w, ts, b, offs, out):
             if a == 0:
                 load_words(PASSES - 1, last_window)
         picked_scales = planes[:].bitcast(U8)
+        bias = keep.tile([P, 1], F32, name="bias")
+        nc.sync.dma_start(out=bias[:], in_=b.rearrange("(p o) -> p o", o=1))
 
         acc = [psum.tile([M, N_TILE], F32, name=f"acc{c}") for c in range(BANKS)]
         sums = keep.tile([M, S], F32, name="sums", align_bytes=64)
@@ -144,36 +146,37 @@ def tile_list_tabts_silu_kernel(tc, tab_words, tab_scales, w, ts, b, offs, out):
 
         gather_words(0, 0, HALF, "words_then_codes")
 
-        w_woven = keep.tile([P, M, PACK], F32, name="w_woven", align_bytes=64)
+        w_woven = keep.tile([P, M, PACK], F32, name="w_woven", tag="woven_then_weights", align_bytes=64)
         upper = keep.tile([P, PASSES, M, PACK], BF16, name="upper", align_bytes=64)
+        rest_woven = keep.tile([P, PASSES - 1, M, PACK], F32, name="rest_woven", align_bytes=64)
+        woven = [w_woven[:], rest_woven[:, 0], rest_woven[:, 1]]
         for a in range(PASSES):
             halves = w_raw[a].bitcast(BF16).rearrange("p i (n t) -> p n i t", t=2)
             nc.scalar.copy(out=upper[:, a], in_=halves[:, :, :, 1])
-            if a == 0:
-                nc.scalar.copy(out=w_woven[:], in_=w_raw[0].rearrange("p i n -> p n i"))
-        rest_woven = keep.tile([P, PASSES - 1, M, PACK], F32, name="rest_woven", align_bytes=64)
-        for j in range(PASSES - 1):
-            nc.scalar.copy(out=rest_woven[:, j], in_=w_raw[1 + j].rearrange("p i n -> p n i"))
+            nc.scalar.copy(out=woven[a], in_=w_raw[a].rearrange("p i n -> p n i"))
         first_bf = keep.tile([P, 2, 1, M, PACK], BF16, name="first_bf", tag="ts_then_weights", align_bytes=64)
-        rest_bf = keep.tile([P, 2, PASSES - 1, M, PACK], BF16, name="rest_bf", align_bytes=64)
 
-        def cut_to_hi(rounded, first, last):
+        def cut_to_hi(rounded, j, a):
             nc.vector.tensor_scalar(
-                out=as_words(rounded[:, 0]),
-                in0=as_words(upper[:, first:last]),
+                out=as_words(rounded[:, 0, j : j + 1]),
+                in0=as_words(upper[:, a : a + 1]),
                 scalar1=PAIR_MASK,
                 scalar2=None,
                 op0=ALU.bitwise_and,
             )
 
-        cut_to_hi(first_bf, 0, 1)
+        cut_to_hi(first_bf, 0, 0)
         nc.gpsimd.tensor_tensor(first_bf[:, 1, 0], w_woven[:], first_bf[:, 0, 0], ALU.subtract)
         gather_words(0, HALF, HALF, "w_then_words")
-        cut_to_hi(rest_bf, 1, PASSES)
         quantize_parts([0], first_bf, "first_codes")
 
-        nc.gpsimd.tensor_tensor(rest_bf[:, 1], rest_woven[:], rest_bf[:, 0], ALU.subtract)
-        gather_words(1, 0, S, "picked1")
+        rest_bf = keep.tile([P, 2, PASSES - 1, M, PACK], BF16, name="rest_bf", tag="woven_then_weights", align_bytes=64)
+        cut_to_hi(rest_bf, 0, 1)
+        nc.gpsimd.tensor_tensor(rest_bf[:, 1, 0], woven[1], rest_bf[:, 0, 0], ALU.subtract)
+        gather_words(1, 0, HALF, "picked1")
+        cut_to_hi(rest_bf, 1, 2)
+        nc.gpsimd.tensor_tensor(rest_bf[:, 1, 1], woven[2], rest_bf[:, 0, 1], ALU.subtract)
+        gather_words(1, HALF, HALF, "w_then_words1")
         for c in range(BANKS):
             multiply(0, c)
         quantize_parts([1, 2], rest_bf, "words_then_codes")

@@ -27,8 +27,10 @@ QUADRANT = 32
 ROWS = 4
 TURNS = 4
 PAIR_MASK = -0x000F0010
+CUT = 2.0**20
+MIDDLE = 15 / 32
 FIRST_ROW = (0, 16, 112)
-OUT_WIDTHS = (512, 512, 512, 320, 192)
+OUT_WIDTHS = (512, 512, 512, 256, 128, 128)
 
 
 def tile_list_tabts_silu_kernel(tc, tab_words, tab_scales, w, ts, b, offs, out):
@@ -61,7 +63,7 @@ def tile_list_tabts_silu_kernel(tc, tab_words, tab_scales, w, ts, b, offs, out):
         w_second = keep.tile([P, PACK, M], F32, name="w_second", align_bytes=64)
         nc.sync.dma_start(out=w_second[:].rearrange("p i n -> p (i n)"), in_=w_rows[:, 1])
         load_words(1, word_window[1])
-        w_third = keep.tile([P, PACK, M], F32, name="w_third", tag="w_then_words1", align_bytes=64)
+        w_third = keep.tile([P, PACK, M], F32, name="w_third", align_bytes=64)
         nc.sync.dma_start(out=w_third[:].rearrange("p i n -> p (i n)"), in_=w_rows[:, 2])
         w_raw = [w_first[:], w_second[:], w_third[:]]
 
@@ -96,8 +98,6 @@ def tile_list_tabts_silu_kernel(tc, tab_words, tab_scales, w, ts, b, offs, out):
             if a == 0:
                 load_words(PASSES - 1, last_window)
         picked_scales = planes[:].bitcast(U8)
-        bias = keep.tile([P, 1], F32, name="bias")
-        nc.sync.dma_start(out=bias[:], in_=b.rearrange("(p o) -> p o", o=1))
 
         acc = [psum.tile([M, N_TILE], F32, name=f"acc{c}") for c in range(BANKS)]
         sums = keep.tile([M, S], F32, name="sums", align_bytes=64)
@@ -142,41 +142,47 @@ def tile_list_tabts_silu_kernel(tc, tab_words, tab_scales, w, ts, b, offs, out):
                     w_codes[a, part], w_scales[a, part] = codes[:, part, j], scales[:, part, j]
 
         def as_words(pairs):
-            return pairs.rearrange("p a n i -> p (a n i)").bitcast(I32)
+            return pairs.rearrange("p n i -> p (n i)").bitcast(I32)
+
+        def upper_halves(a):
+            return w_raw[a].bitcast(BF16).rearrange("p i (n t) -> p n i t", t=2)[:, :, :, 1]
 
         gather_words(0, 0, HALF, "words_then_codes")
 
-        w_woven = keep.tile([P, M, PACK], F32, name="w_woven", tag="woven_then_weights", align_bytes=64)
-        upper = keep.tile([P, PASSES, M, PACK], BF16, name="upper", align_bytes=64)
-        rest_woven = keep.tile([P, PASSES - 1, M, PACK], F32, name="rest_woven", align_bytes=64)
-        woven = [w_woven[:], rest_woven[:, 0], rest_woven[:, 1]]
-        for a in range(PASSES):
-            halves = w_raw[a].bitcast(BF16).rearrange("p i (n t) -> p n i t", t=2)
-            nc.scalar.copy(out=upper[:, a], in_=halves[:, :, :, 1])
-            nc.scalar.copy(out=woven[a], in_=w_raw[a].rearrange("p i n -> p n i"))
+        w_woven = keep.tile([P, M, PACK], F32, name="w_woven", align_bytes=64)
+        upper = keep.tile([P, M, PACK], BF16, name="upper", tag="upper_then_bias", align_bytes=64)
+        nc.scalar.copy(out=upper[:], in_=upper_halves(0))
+        nc.scalar.copy(out=w_woven[:], in_=w_raw[0].rearrange("p i n -> p n i"))
         first_bf = keep.tile([P, 2, 1, M, PACK], BF16, name="first_bf", tag="ts_then_weights", align_bytes=64)
-
-        def cut_to_hi(rounded, j, a):
-            nc.vector.tensor_scalar(
-                out=as_words(rounded[:, 0, j : j + 1]),
-                in0=as_words(upper[:, a : a + 1]),
-                scalar1=PAIR_MASK,
-                scalar2=None,
-                op0=ALU.bitwise_and,
-            )
-
-        cut_to_hi(first_bf, 0, 0)
+        nc.vector.tensor_scalar(
+            out=as_words(first_bf[:, 0, 0]),
+            in0=as_words(upper[:]),
+            scalar1=PAIR_MASK,
+            scalar2=None,
+            op0=ALU.bitwise_and,
+        )
         nc.gpsimd.tensor_tensor(first_bf[:, 1, 0], w_woven[:], first_bf[:, 0, 0], ALU.subtract)
         gather_words(0, HALF, HALF, "w_then_words")
         quantize_parts([0], first_bf, "first_codes")
+        bias = keep.tile([P, 1], F32, name="bias", tag="upper_then_bias", align_bytes=64)
+        nc.sync.dma_start(out=bias[:], in_=b.rearrange("(p o) -> p o", o=1))
 
-        rest_bf = keep.tile([P, 2, PASSES - 1, M, PACK], BF16, name="rest_bf", tag="woven_then_weights", align_bytes=64)
-        cut_to_hi(rest_bf, 0, 1)
-        nc.gpsimd.tensor_tensor(rest_bf[:, 1, 0], woven[1], rest_bf[:, 0, 0], ALU.subtract)
-        gather_words(1, 0, HALF, "picked1")
-        cut_to_hi(rest_bf, 1, 2)
-        nc.gpsimd.tensor_tensor(rest_bf[:, 1, 1], woven[2], rest_bf[:, 0, 1], ALU.subtract)
-        gather_words(1, HALF, HALF, "w_then_words1")
+        rest_bf = keep.tile([P, 2, PASSES - 1, M, PACK], BF16, name="rest_bf", tag="ts_then_weights", align_bytes=64)
+        rest_hi = keep.tile([P, PASSES - 1, M, PACK], U32, name="rest_hi", align_bytes=64)
+        for a in range(1, PASSES):
+            wide = keep.tile([P, M, PACK], F32, name=f"wide{a}", align_bytes=64)
+            top = keep.tile([P, M, PACK], U32, name=f"top{a}", align_bytes=64)
+            hi = rest_hi[:, a - 1]
+            w_by_column = w_raw[a].rearrange("p i n -> p n i")
+            for n in (slice(0, M // 2), slice(M // 2, M)):
+                nc.scalar.copy(out=wide[:, n], in_=upper_halves(a)[:, n])
+                nc.scalar.activation(
+                    out=top[:, n], in_=wide[:, n].bitcast(U32), func=ACT.Copy, scale=1 / CUT, bias=-MIDDLE
+                )
+                nc.scalar.activation(out=hi[:, n], in_=top[:, n], func=ACT.Copy, scale=CUT)
+                nc.gpsimd.tensor_tensor(rest_bf[:, 1, a - 1, n], w_by_column[:, n], hi[:, n].bitcast(F32), ALU.subtract)
+        nc.scalar.copy(out=rest_bf[:, 0], in_=rest_hi[:].bitcast(F32))
+        gather_words(1, 0, S, "picked1")
         for c in range(BANKS):
             multiply(0, c)
         quantize_parts([1, 2], rest_bf, "words_then_codes")

@@ -30,7 +30,7 @@ PAIR_MASK = -0x000F0010
 CUT = 2.0**20
 MIDDLE = 15 / 32
 FIRST_ROW = (0, 16, 112)
-OUT_WIDTHS = (512, 512, 512, 256, 128, 128)
+OUT_WIDTHS = (512, 512, 416, 288, 192, 128)
 
 
 def tile_list_tabts_silu_kernel(tc, tab_words, tab_scales, w, ts, b, offs, out):

@@ -172,7 +172,7 @@ def tile_list_tabts_silu_kernel(tc, tab_words, tab_scales, w, ts, b, offs, out):
         for a in range(1, PASSES):
             wide = keep.tile([P, M, PACK], F32, name=f"wide{a}", align_bytes=64)
             top = keep.tile([P, M, PACK], U32, name=f"top{a}", align_bytes=64)
-            hi = rest_hi[:, a - 1]
+            hi, lo = rest_hi[:, a - 1], rest_bf[:, 1, a - 1]
             w_by_column = w_raw[a].rearrange("p i n -> p n i")
             for n in (slice(0, M // 2), slice(M // 2, M)):
                 nc.scalar.copy(out=wide[:, n], in_=upper_halves(a)[:, n])
@@ -180,7 +180,12 @@ def tile_list_tabts_silu_kernel(tc, tab_words, tab_scales, w, ts, b, offs, out):
                     out=top[:, n], in_=wide[:, n].bitcast(U32), func=ACT.Copy, scale=1 / CUT, bias=-MIDDLE
                 )
                 nc.scalar.activation(out=hi[:, n], in_=top[:, n], func=ACT.Copy, scale=CUT)
-                nc.gpsimd.tensor_tensor(rest_bf[:, 1, a - 1, n], w_by_column[:, n], hi[:, n].bitcast(F32), ALU.subtract)
+                if a == PASSES - 1:
+                    nc.gpsimd.tensor_tensor(lo[:, n], w_by_column[:, n], hi[:, n].bitcast(F32), ALU.subtract)
+            if a < PASSES - 1:
+                second_woven = keep.tile([P, M, PACK], F32, name="second_woven", align_bytes=64)
+                nc.scalar.copy(out=second_woven[:], in_=w_by_column)
+                nc.gpsimd.tensor_tensor(lo, second_woven[:], hi.bitcast(F32), ALU.subtract)
         nc.scalar.copy(out=rest_bf[:, 0], in_=rest_hi[:].bitcast(F32))
         gather_words(1, 0, S, "picked1")
         for c in range(BANKS):

@@ -37,6 +37,7 @@ def tile_list_tabts_silu_kernel(tc, tab_words, tab_scales, w, ts, b, offs, out):
     nc = tc.nc
     with ExitStack() as ctx:
         keep = ctx.enter_context(tc.tile_pool(name="keep", bufs=1))
+        zeroed = ctx.enter_context(tc.tile_pool(name="zeroed", bufs=1))
         psum = ctx.enter_context(tc.psum_pool(name="psum", bufs=1))
         turn = ctx.enter_context(tc.psum_pool(name="turn", bufs=4))
 
@@ -69,10 +70,11 @@ def tile_list_tabts_silu_kernel(tc, tab_words, tab_scales, w, ts, b, offs, out):
 
         identity = keep.tile([P, P], F32, name="identity", align_bytes=64)
         make_identity(nc, identity[:])
-        warm = keep.tile([P, 1], F32, name="warm", tag="warm_then_planes", align_bytes=64)
-        nc.scalar.activation(out=warm[:], in_=identity[:, 0:1], func=ACT.Silu)
-        planes = keep.tile([P, PASSES, S // 4], I32, name="planes", tag="warm_then_planes", align_bytes=64)
-        nc.gpsimd.memset(planes[:].rearrange("p a s -> p (a s)"), 0)
+        warm = zeroed.tile([P, PASSES * S // 4], F32, name="warm", offset=0, align_bytes=64)
+        nc.scalar.activation(out=warm[:, 0:1], in_=identity[:, 0:1], func=ACT.Silu)
+        planes = [zeroed.tile([P, S // 4], I32, name=f"plane{a}", offset=a * S, align_bytes=64) for a in range(PASSES)]
+        for plane in planes:
+            nc.gpsimd.memset(plane[:], 0)
 
         picked_rows = keep.tile([P, S], U8, name="picked_rows", align_bytes=64)
         nc.vector.tensor_copy(picked_rows[:], scale_window[:].bitcast(U8).indirect(offsets[:]))
@@ -89,15 +91,14 @@ def tile_list_tabts_silu_kernel(tc, tab_words, tab_scales, w, ts, b, offs, out):
         last_window = keep.tile([P, T], I32, name="last_window", tag="scales_then_words", align_bytes=64)
         word_window.append(last_window)
         for a in range(PASSES):
-            for quad in range(P // QUADRANT):
-                row = FIRST_ROW[a] + ROWS * quad
+            for r in range(ROWS):
+                row = FIRST_ROW[a] + r
                 nc.sync.dma_start(
-                    out=planes[QUADRANT * quad : QUADRANT * quad + ROWS, a, :],
-                    in_=picked_rows[row : row + ROWS, :].bitcast(I32),
+                    out=planes[a][ROWS * a + r :: QUADRANT, :],
+                    in_=picked_rows[row : row + 3 * ROWS + 1 : ROWS, :].bitcast(I32),
                 )
             if a == 0:
                 load_words(PASSES - 1, last_window)
-        picked_scales = planes[:].bitcast(U8)
 
         acc = [psum.tile([M, N_TILE], F32, name=f"acc{c}") for c in range(BANKS)]
         sums = keep.tile([M, S], F32, name="sums", align_bytes=64)
@@ -123,7 +124,7 @@ def tile_list_tabts_silu_kernel(tc, tab_words, tab_scales, w, ts, b, offs, out):
                     lhsT=w_codes[a, part].bitcast(FP8X4),
                     lhsT_scale=w_scales[a, part],
                     rhs=picked[a, c].bitcast(FP8X4),
-                    rhs_scale=picked_scales[:, a, cols],
+                    rhs_scale=planes[a][ROWS * a :, :].bitcast(U8)[:, cols],
                     start=(a == 0 and part == 0),
                     stop=(a == PASSES - 1 and part == 1),
                 )

@@ -1,7 +1,6 @@
 from contextlib import ExitStack
 
 import concourse.mybir as mybir
-from concourse.masks import make_identity
 
 K, M, T, S = 1536, 128, 4096, 2048
 FLOPS = 2 * 2 * K * M * S
@@ -44,6 +43,8 @@ def tile_list_tabts_silu_kernel(tc, tab_words, tab_scales, w, ts, b, offs, out):
         offsets = keep.tile([P, S // PER_COL], U16, name="offsets")
         scale_window = keep.tile([P, T // 4], I32, name="scale_window", tag="scales_then_words", align_bytes=64)
         nc.vector.memset(scale_window[QUADRANT : 2 * QUADRANT, :], 0)
+        zeros = zeroed.tile([P, PASSES * S // 4], F32, name="zeros", offset=0, align_bytes=64)
+        nc.vector.memset(zeros[:, :P], 0.0)
         nc.vector.memset(scale_window[2 * QUADRANT : FIRST_ROW[2], :], 0)
 
         scale_rows = tab_scales.rearrange("a q t -> (a q) t").bitcast(I32)
@@ -69,9 +70,17 @@ def tile_list_tabts_silu_kernel(tc, tab_words, tab_scales, w, ts, b, offs, out):
         w_raw = [w_first[:], w_second[:], w_third[:]]
 
         identity = keep.tile([P, P], F32, name="identity", align_bytes=64)
-        make_identity(nc, identity[:])
-        warm = zeroed.tile([P, PASSES * S // 4], F32, name="warm", offset=0, align_bytes=64)
-        nc.scalar.activation(out=warm[:, 0:1], in_=identity[:, 0:1], func=ACT.Silu)
+        nc.gpsimd.affine_select(
+            out=identity[:],
+            in_=zeros[:, :P],
+            compare_op=ALU.not_equal,
+            fill=1.0,
+            base=0,
+            pattern=[[-1, P]],
+            channel_multiplier=1,
+        )
+        warm = keep.tile([P, 1], F32, name="warm", align_bytes=64)
+        nc.scalar.activation(out=warm[:], in_=identity[:, 0:1], func=ACT.Silu)
         planes = [zeroed.tile([P, S // 4], I32, name=f"plane{a}", offset=a * S, align_bytes=64) for a in range(PASSES)]
         for plane in planes:
             nc.gpsimd.memset(plane[:], 0)
@@ -95,7 +104,7 @@ def tile_list_tabts_silu_kernel(tc, tab_words, tab_scales, w, ts, b, offs, out):
                 row = FIRST_ROW[a] + r
                 nc.sync.dma_start(
                     out=planes[a][ROWS * a + r :: QUADRANT, :],
-                    in_=picked_rows[row : row + 3 * ROWS + 1 : ROWS, :].bitcast(I32),
+                    in_=picked_rows[row : row + (P // QUADRANT - 1) * ROWS + 1 : ROWS, :].bitcast(I32),
                 )
             if a == 0:
                 load_words(PASSES - 1, last_window)

@@ -30,6 +30,7 @@ CUT = 2.0**20
 MIDDLE = 15 / 32
 FIRST_ROW = (0, 16, 112)
 OUT_WIDTHS = (512, 512, 416, 288, 192, 128)
+HALVED = OUT_WIDTHS[2:4]
 
 
 def tile_list_tabts_silu_kernel(tc, tab_words, tab_scales, w, ts, b, offs, out):
@@ -220,6 +221,9 @@ def tile_list_tabts_silu_kernel(tc, tab_words, tab_scales, w, ts, b, offs, out):
             nc.vector.tensor_tensor(
                 scaled[:, cols], ts_window[:].indirect(list_slice(start, width)), sums[:, cols], ALU.mult
             )
-            nc.scalar.activation(out=result[:, cols], in_=scaled[:, cols], func=ACT.Silu, bias=bias[:])
-            nc.sync.dma_start(out=out[:, cols], in_=result[:, cols])
+            parts = 2 if width in HALVED else 1
+            for first in range(start, start + width, width // parts):
+                part = slice(first, first + width // parts)
+                nc.scalar.activation(out=result[:, part], in_=scaled[:, part], func=ACT.Silu, bias=bias[:])
+                nc.sync.dma_start(out=out[:, part], in_=result[:, part])
             start += width

from contextlib import ExitStack

import concourse.mybir as mybir

K, M, T, S = 1536, 128, 4096, 2048
FLOPS = 2 * 2 * K * M * S

F32 = mybir.dt.float32
BF16 = mybir.dt.bfloat16
I32 = mybir.dt.int32
U32 = mybir.dt.uint32
U16 = mybir.dt.uint16
U8 = mybir.dt.uint8
FP8X4 = mybir.dt.float8_e4m3fn_x4
ALU = mybir.AluOpType
ACT = mybir.ActivationFunctionType

P = 128
PACK = 4
PASSES = K // (P * PACK)
N_TILE = 512
BANKS = S // N_TILE
HALF = S // 2
PER_COL = 16
QUADRANT = 32
ROWS = 4
TURNS = 4
PAIR_MASK = -0x000F0010
CUT = 2.0**20
MIDDLE = 15 / 32
FIRST_ROW = (0, 16, 112)
OUT_WIDTHS = (512, 512, 416, 288, 192, 128)
HALVED = OUT_WIDTHS[2:4]


def tile_list_tabts_silu_kernel(tc, tab_words, tab_scales, w, ts, b, offs, out):
    nc = tc.nc
    with ExitStack() as ctx:
        keep = ctx.enter_context(tc.tile_pool(name="keep", bufs=1))
        zeroed = ctx.enter_context(tc.tile_pool(name="zeroed", bufs=1))
        psum = ctx.enter_context(tc.psum_pool(name="psum", bufs=1))
        turn = ctx.enter_context(tc.psum_pool(name="turn", bufs=4))

        offsets = keep.tile([P, S // PER_COL], U16, name="offsets")
        scale_window = keep.tile([P, T // 4], I32, name="scale_window", tag="scales_then_words", align_bytes=64)
        nc.vector.memset(scale_window[QUADRANT : 2 * QUADRANT, :], 0)
        zeros = zeroed.tile([P, PASSES * S // 4], F32, name="zeros", offset=0, align_bytes=64)
        nc.vector.memset(zeros[:, :P], 0.0)
        nc.vector.memset(scale_window[2 * QUADRANT : FIRST_ROW[2], :], 0)

        scale_rows = tab_scales.rearrange("a q t -> (a q) t").bitcast(I32)
        nc.sync.dma_start(out=scale_window[0:QUADRANT, :], in_=scale_rows[0:QUADRANT, :])
        nc.sync.dma_start(out=scale_window[FIRST_ROW[2] :, :], in_=scale_rows[QUADRANT:, :])
        nc.sync.dma_start(offsets[:], offs)
        ts_rows = keep.tile([P, T // P], F32, name="ts_rows", tag="ts_then_weights", align_bytes=64)
        nc.sync.dma_start(out=ts_rows[:], in_=ts[0].rearrange("(p c) -> p c", p=P))

        def load_words(a, window):
            nc.sync.dma_start(out=window[:], in_=tab_words[a].rearrange("p t i -> p (t i)").bitcast(I32))

        word_window = [keep.tile([P, T], I32, name=f"word_window{a}", align_bytes=64) for a in range(PASSES - 1)]
        load_words(0, word_window[0])
        w_rows = w.rearrange("(a p i) n -> p a (i n)", p=P, i=PACK)
        w_first = keep.tile([P, PACK, M], F32, name="w_first", tag="w_then_words", align_bytes=64)
        nc.sync.dma_start(out=w_first[:].rearrange("p i n -> p (i n)"), in_=w_rows[:, 0])
        w_second = keep.tile([P, PACK, M], F32, name="w_second", align_bytes=64)
        nc.sync.dma_start(out=w_second[:].rearrange("p i n -> p (i n)"), in_=w_rows[:, 1])
        load_words(1, word_window[1])
        w_third = keep.tile([P, PACK, M], F32, name="w_third", align_bytes=64)
        nc.sync.dma_start(out=w_third[:].rearrange("p i n -> p (i n)"), in_=w_rows[:, 2])
        w_raw = [w_first[:], w_second[:], w_third[:]]

        identity = keep.tile([P, P], F32, name="identity", align_bytes=64)
        nc.gpsimd.affine_select(
            out=identity[:],
            in_=zeros[:, :P],
            compare_op=ALU.not_equal,
            fill=1.0,
            base=0,
            pattern=[[-1, P]],
            channel_multiplier=1,
        )
        warm = keep.tile([P, 1], F32, name="warm", align_bytes=64)
        nc.scalar.activation(out=warm[:], in_=identity[:, 0:1], func=ACT.Silu)
        planes = [zeroed.tile([P, S // 4], I32, name=f"plane{a}", offset=a * S, align_bytes=64) for a in range(PASSES)]
        for plane in planes:
            nc.gpsimd.memset(plane[:], 0)

        picked_rows = keep.tile([P, S], U8, name="picked_rows", align_bytes=64)
        nc.vector.tensor_copy(picked_rows[:], scale_window[:].bitcast(U8).indirect(offsets[:]))

        ts_window = keep.tile([P, T], F32, name="ts_window", align_bytes=64)
        ts_by_row = ts_window[:].rearrange("p (r c) -> p r c", r=P)
        for c0 in range(0, T // P, TURNS):
            bank = turn.tile([P, TURNS, P], F32, name="bank")
            for j in range(TURNS):
                column = ts_rows[:, c0 + j : c0 + j + 1]
                nc.tensor.transpose(bank[:, j, :], column.to_broadcast([P, P]), identity[:])
            nc.scalar.copy(out=ts_by_row[:, :, c0 : c0 + TURNS], in_=bank[:].rearrange("p j r -> p r j"))

        last_window = keep.tile([P, T], I32, name="last_window", tag="scales_then_words", align_bytes=64)
        word_window.append(last_window)
        for a in range(PASSES):
            for r in range(ROWS):
                row = FIRST_ROW[a] + r
                nc.sync.dma_start(
                    out=planes[a][ROWS * a + r :: QUADRANT, :],
                    in_=picked_rows[row : row + (P // QUADRANT - 1) * ROWS + 1 : ROWS, :].bitcast(I32),
                )
            if a == 0:
                load_words(PASSES - 1, last_window)

        acc = [psum.tile([M, N_TILE], F32, name=f"acc{c}") for c in range(BANKS)]
        sums = keep.tile([M, S], F32, name="sums", align_bytes=64)

        def list_slice(start, width):
            return offsets[:, start // PER_COL : (start + width) // PER_COL]

        picked = {}

        def gather_words(a, start, width, tag):
            tile = keep.tile([P, width], U32, name=f"picked{a}_{start}", tag=tag, align_bytes=64)
            nc.vector.tensor_copy(tile[:], word_window[a][:].bitcast(U32).indirect(list_slice(start, width)))
            for c in range(width // N_TILE):
                picked[a, start // N_TILE + c] = tile[:, c * N_TILE : (c + 1) * N_TILE]

        w_codes, w_scales = {}, {}

        def multiply(a, c):
            cols = slice(c * N_TILE, (c + 1) * N_TILE)
            for part in range(2):
                nc.tensor.matmul_mx(
                    out=acc[c][:],
                    lhsT=w_codes[a, part].bitcast(FP8X4),
                    lhsT_scale=w_scales[a, part],
                    rhs=picked[a, c].bitcast(FP8X4),
                    rhs_scale=planes[a][ROWS * a :, :].bitcast(U8)[:, cols],
                    start=(a == 0 and part == 0),
                    stop=(a == PASSES - 1 and part == 1),
                )

        def quantize_parts(passes, rounded, tag):
            count = len(passes)
            codes = keep.tile([P, 2, count, M], U32, name=f"w_codes{passes[0]}", tag=tag, align_bytes=64)
            scales = keep.tile([P, 2, count, M], U8, name=f"w_scales{passes[0]}", align_bytes=64)
            nc.vector.quantize_mx(
                out=codes[:].rearrange("p h a n -> p (h a n)").bitcast(FP8X4),
                scales=scales[:].rearrange("p h a n -> p (h a n)"),
                in_=rounded[:].rearrange("p h a n i -> p (h a n i)"),
            )
            for j, a in enumerate(passes):
                for part in range(2):
                    w_codes[a, part], w_scales[a, part] = codes[:, part, j], scales[:, part, j]

        def as_words(pairs):
            return pairs.rearrange("p n i -> p (n i)").bitcast(I32)

        def upper_halves(a):
            return w_raw[a].bitcast(BF16).rearrange("p i (n t) -> p n i t", t=2)[:, :, :, 1]

        gather_words(0, 0, HALF, "words_then_codes")

        w_woven = keep.tile([P, M, PACK], F32, name="w_woven", align_bytes=64)
        upper = keep.tile([P, M, PACK], BF16, name="upper", tag="upper_then_bias", align_bytes=64)
        nc.scalar.copy(out=upper[:], in_=upper_halves(0))
        nc.scalar.copy(out=w_woven[:], in_=w_raw[0].rearrange("p i n -> p n i"))
        first_bf = keep.tile([P, 2, 1, M, PACK], BF16, name="first_bf", tag="ts_then_weights", align_bytes=64)
        nc.vector.tensor_scalar(
            out=as_words(first_bf[:, 0, 0]),
            in0=as_words(upper[:]),
            scalar1=PAIR_MASK,
            scalar2=None,
            op0=ALU.bitwise_and,
        )
        nc.gpsimd.tensor_tensor(first_bf[:, 1, 0], w_woven[:], first_bf[:, 0, 0], ALU.subtract)
        gather_words(0, HALF, HALF, "w_then_words")
        quantize_parts([0], first_bf, "first_codes")
        bias = keep.tile([P, 1], F32, name="bias", tag="upper_then_bias", align_bytes=64)
        nc.sync.dma_start(out=bias[:], in_=b.rearrange("(p o) -> p o", o=1))

        rest_bf = keep.tile([P, 2, PASSES - 1, M, PACK], BF16, name="rest_bf", tag="ts_then_weights", align_bytes=64)
        rest_hi = keep.tile([P, PASSES - 1, M, PACK], U32, name="rest_hi", align_bytes=64)
        for a in range(1, PASSES):
            wide = keep.tile([P, M, PACK], F32, name=f"wide{a}", align_bytes=64)
            top = keep.tile([P, M, PACK], U32, name=f"top{a}", align_bytes=64)
            hi, lo = rest_hi[:, a - 1], rest_bf[:, 1, a - 1]
            w_by_column = w_raw[a].rearrange("p i n -> p n i")
            for n in (slice(0, M // 2), slice(M // 2, M)):
                nc.scalar.copy(out=wide[:, n], in_=upper_halves(a)[:, n])
                nc.scalar.activation(
                    out=top[:, n], in_=wide[:, n].bitcast(U32), func=ACT.Copy, scale=1 / CUT, bias=-MIDDLE
                )
                nc.scalar.activation(out=hi[:, n], in_=top[:, n], func=ACT.Copy, scale=CUT)
                if a == PASSES - 1:
                    nc.gpsimd.tensor_tensor(lo[:, n], w_by_column[:, n], hi[:, n].bitcast(F32), ALU.subtract)
            if a < PASSES - 1:
                second_woven = keep.tile([P, M, PACK], F32, name="second_woven", align_bytes=64)
                nc.scalar.copy(out=second_woven[:], in_=w_by_column)
                nc.gpsimd.tensor_tensor(lo, second_woven[:], hi.bitcast(F32), ALU.subtract)
        nc.scalar.copy(out=rest_bf[:, 0], in_=rest_hi[:].bitcast(F32))
        gather_words(1, 0, S, "picked1")
        for c in range(BANKS):
            multiply(0, c)
        quantize_parts([1, 2], rest_bf, "words_then_codes")

        for start in range(0, S, HALF):
            gather_words(PASSES - 1, start, HALF, f"picked2_{start}")
            banks = range(start // N_TILE, (start + HALF) // N_TILE)
            for c in banks:
                multiply(1, c)
            for c in banks:
                multiply(PASSES - 1, c)
                cols = slice(c * N_TILE, (c + 1) * N_TILE)
                nc.scalar.activation(out=sums[:, cols], in_=acc[c][:], func=ACT.Copy)

        scaled = keep.tile([M, S], F32, name="scaled", align_bytes=64)
        result = keep.tile([M, S], F32, name="result", align_bytes=64)
        start = 0
        for width in OUT_WIDTHS:
            cols = slice(start, start + width)
            nc.vector.tensor_tensor(
                scaled[:, cols], ts_window[:].indirect(list_slice(start, width)), sums[:, cols], ALU.mult
            )
            parts = 2 if width in HALVED else 1
            for first in range(start, start + width, width // parts):
                part = slice(first, first + width // parts)
                nc.scalar.activation(out=result[:, part], in_=scaled[:, part], func=ACT.Silu, bias=bias[:])
                nc.sync.dma_start(out=out[:, part], in_=result[:, part])
            start += width
